import numpy as np, ml_dtypes
CORES = [3,11,19,27,35,43]
N = 6
BF = ml_dtypes.bfloat16
def gentries(a):
    return np.ascontiguousarray(a.reshape(8, 16, -1).transpose(0, 2, 1)).reshape(8, -1)
def gtable(e):
    e = np.asarray(e); return np.ascontiguousarray(e.reshape(8, -1, 16).transpose(0, 2, 1)).reshape(128, -1).astype(np.int32)
E, LEN, NC, RO, DR, DG = 2048, 8, 512, 5, 1, 3
MOD = (4, 4, 4, 2)
KINDS = np.array([1, 1, 2, 15, 16]); WAYS = np.array([0, 1, 2]); ROWS16 = np.arange(16)
def some(rng, kd, rows):
    i = rng.choice(rows, kd.shape); j = (i + rng.integers(1, 16, kd.shape)) & 15; row = np.arange(16).reshape(1, 1, 16, 1)
    return np.where(kd == 1, row == i, np.where(kd == 2, (row == i) | (row == j), (kd == 16) | (row != i))), row == i
def soil(rng, s, x, rate, kinds, ways, rows):
    sh = x.shape[:2] + (1, x.shape[3]); hit = rng.random(sh) < rate; on, first = some(rng, rng.choice(kinds, sh), rows); on = on & hit
    way = rng.choice(ways, sh); dl = rng.integers(1, 4, sh) * (2 * rng.integers(0, 2, sh) - 1); dl = np.where(first, dl, -dl)
    y = x + dl; y = np.where(np.abs(y) > 7, x - dl, y)
    return np.where(on & (way != 1), -s, s), np.where(on & (way != 0), y, x)
def graph(rng):
    A = E // 16; a = np.arange(A); nx = np.zeros((A, 8), np.int64); w = 1
    for i in range(4):
        m = MOD[i]; z = (a // w) % m
        nx[:, 2 * i] = a + ((z + 1) % m - z) * w; nx[:, 2 * i + 1] = a + ((z - 1) % m - z) * w; w *= m
    tau = np.argsort(rng.random((A, 8)), axis=1); inv = np.argsort(tau, axis=1); hi = np.argsort(rng.random((8, E // 8)), axis=1)
    nm = 8 * hi[tau[:, :, None], 2 * a[:, None, None] + np.arange(2)] + tau[:, :, None]
    at = np.zeros(E, np.int64); dr = np.zeros(E, np.int64); at[nm] = a[:, None, None]; dr[nm] = np.arange(8)[None, :, None]
    far = nx[at, dr]; j = np.ascontiguousarray(inv[far].T)
    sq = np.concatenate([nm[at, j, rng.integers(0, 2, (8, E))], nm[nx[at, j], dr, rng.integers(0, 2, (8, E))]])
    h = rng.integers(0, 8, (N, 8, NC, LEN // 2)); d = np.concatenate([h, h ^ 1], axis=3); d = np.take_along_axis(d, np.argsort(rng.random(d.shape), axis=3), 3)
    c = np.zeros(d.shape, np.int64); p = rng.integers(0, A, (N, 8, NC)); t = rng.integers(0, 2, d.shape)
    for i in range(LEN):
        c[..., i] = nm[p, d[..., i], t[..., i]]; p = nx[p, d[..., i]]
    sg = 2 * rng.integers(0, 2, (N, 8, 16, A)) - 1; u = rng.integers(0, 8, (N, 8, 16, A))
    return sg[..., at] * sg[..., far], sg[..., at] * (u[..., at] - u[..., far]), sq, c
def pack(s, x, sq, c):
    return {"v": np.ascontiguousarray((16 * s + x).reshape(N, 128, E)).astype(np.float32).astype(BF), "sq": np.stack([sq] * N).astype(np.int32), "lp": np.stack([gtable(a.reshape(8, -1)) for a in c])}
def skew(rng, shape, w):
    z = (E * rng.random(shape) ** w).astype(np.int64)
    return np.where(rng.random(shape) < 0.5, z, E - 1 - z)
def signs(rng, *shape):
    return 2 * rng.integers(0, 2, shape) - 1
def setup_inputs(rng):
    s, x, sq, c = graph(rng)
    s, x = soil(rng, s, x, rng.choice(np.array([0.03, 0.08, 0.15, 0.22]), (N, 8, 1, 1)), KINDS, WAYS, ROWS16)
    return pack(s, x, sq, c)
def setup_inputs_near(rng):
    s, x, sq, c = graph(rng)
    for b, kinds, ways, rows in ((0, [1], [0], [15]), (1, [2], [1], list(range(16))), (2, [1], [1], [0, 7, 8, 15]), (3, [15, 16], [0, 1, 2], list(range(16)))):
        s[:, b::4], x[:, b::4] = soil(rng, s[:, b::4], x[:, b::4], 0.15, np.array(kinds), np.array(ways), np.array(rows))
    return pack(s, x, sq, c)
def setup_inputs_spread(rng):
    s = np.repeat(signs(rng, N, 8, 16, 1), 5, axis=3); x = np.repeat(rng.integers(-7, 8, (N, 8, 16, 1)), 5, axis=3)
    s[..., 1:3], x[..., 1:3] = soil(rng, s[..., 1:3], x[..., 1:3], 1.0, KINDS, WAYS, ROWS16)
    s[..., 3:] = signs(rng, N, 8, 16, 2); x[..., 3:] = rng.integers(-7, 8, (N, 8, 16, 2))
    who = (5 * rng.random((N, 8, E)) ** rng.choice(np.array([4.0, 8.0, 16.0]), (N, 8, 1))).astype(np.int64)[:, :, None, :]
    w = np.array([1.0, 2.0, 4.0])
    return pack(np.take_along_axis(s, who, 3), np.take_along_axis(x, who, 3), skew(rng, (16, E), rng.choice(w, (16, 1))), skew(rng, (N, 8, NC, LEN), rng.choice(w, (N, 8, 1, 1))))
def setup_inputs_ends(rng):
    M = E - 1; s0 = signs(rng, N, 8, 16, 1); x0 = 7 * s0 * np.where(rng.random(s0.shape) < 0.85, 1, -1)
    kd = rng.choice(np.array([1, 2, 15, 16]), (N, 8, 1, 2)); on, first = some(rng, kd, ROWS16); way = rng.integers(0, 3, kd.shape)
    s = np.concatenate([s0, np.where(on & (way != 2), -s0, s0)], axis=3); x = np.concatenate([x0, np.where(on & (way != 1), -x0, x0)], axis=3)
    who = rng.choice(np.array([0, 1, 2]), (N, 8, E), p=[0.7, 0.15, 0.15]); q = np.arange(N)[:, None]
    who[..., 0] = 0; who[..., M] = np.where((q + np.arange(8)) % 4 == 3, 1 + (q & 1), 0)
    s = np.take_along_axis(s, who[:, :, None, :], 3); x = np.take_along_axis(x, who[:, :, None, :], 3)
    s[:, 7, 15] = 1; x[:, 7, 15] = 7; s[:, 7, 0] = 1; x[:, 7, 0] = -7
    sq = np.where(rng.random((16, E)) < 0.72, M * rng.integers(0, 2, (16, E)), rng.integers(0, E, (16, E)))
    for e, k, f2, e2 in ((0, 0, 0, M), (0, 7, M, M), (M, 7, M, 0), (M, 0, 0, 0)):
        sq[k, e] = f2; sq[8 + k, e] = e2
    c = np.where(rng.random((N, 8, NC, LEN)) < 0.72, M * rng.integers(0, 2, (N, 8, NC, LEN)), rng.integers(0, E, (N, 8, NC, LEN)))
    return pack(s, x, sq, c)
def setup_inputs_corners(rng):
    M = E - 1; e = np.arange(E); reg = ((np.arange(N)[:, None] + np.arange(8) + rng.integers(0, 8)) % 8).reshape(N, 8, 1, 1)
    s = np.repeat(signs(rng, N, 8, 16, 1), E, axis=3); x = np.repeat(rng.integers(-7, 8, (N, 8, 16, 1)), E, axis=3)
    s, x = soil(rng, s, x, np.where(reg == 1, 0.15, 0.0), KINDS, WAYS, ROWS16)
    s, x = soil(rng, s, x, np.where(reg == 3, 0.25, 0.0), np.array([1, 16]), WAYS, ROWS16)
    s = np.where(reg == 2, signs(rng, N, 8, 16, E), s); x = np.where(reg == 2, rng.integers(-7, 8, (N, 8, 16, E)), x)
    row = np.arange(16).reshape(1, 1, 16, 1); own = rng.integers(0, 16, (N, 8, 1, 1)); low = np.minimum(own, 14); odd = (np.arange(N) & 1).reshape(N, 1, 1, 1) == 1
    two = rng.integers(0, 2, (N, 8, 1, E)); three = rng.integers(0, 3, (N, 8, 1, E))
    x = np.where((reg == 4) & (row == own), rng.integers(-3, 4, (N, 8, 1, 1)) + 4 - 8 * two, x)
    m = np.where(odd, rng.integers(1, 8, (N, 8, 1, 1)), 4)
    x = np.where((reg == 5) & (row == low), m * two, x); x = np.where((reg == 5) & (row == low + 1), -two, x); s = np.where((reg == 5) & ((row == low) | (row == low + 1)), 1, s)
    x = np.where((reg == 6) & (row == own), np.where(three > 0, 7, -7), x); s = np.where((reg == 6) & (row == own), np.where(three == 2, -1, 1), s)
    x = np.where((reg == 7) & (row == own), np.where(odd, 6 + two, -6 - two), x); s = np.where((reg == 7) & (row == own), 1, s)
    a = np.stack([e, 0 * e, 0 * e + M, (e + 1) % E, (e - 1) % E])
    sq = np.where(rng.random((16, E)) < 0.4, rng.integers(0, E, (16, E)), a[rng.integers(0, 5, (16, E)), e])
    b = rng.integers(0, E, (N, 8, NC, 1)); i = np.arange(LEN).reshape(1, 1, 1, LEN); z = np.zeros((N, 8, NC, LEN), np.int64)
    c = np.choose(rng.integers(0, 6, (N, 8, NC, 1)), [b + z, M * (i & 1) + z, (b + i) % E, rng.integers(0, E, z.shape), z, z + M])
    return pack(s, x, sq, c)
def setup_inputs_crowd(rng):
    s = np.repeat(signs(rng, N, 8, 16, 1), E, axis=3); x = np.repeat(rng.integers(-7, 8, (N, 8, 16, 1)), E, axis=3)
    s, x = soil(rng, s, x, 0.12, KINDS, WAYS, ROWS16)
    sq = rng.integers(0, E, (16, E)); c = rng.integers(0, E, (N, 8, NC, LEN)); o = int(rng.integers(0, 4))
    for q in range(N):
        for g in range(8):
            m = (q + g + o) % 4; n = rng.integers(0, E, 3)
            if m < 2: c[q, g] = n[0]
            if m == 1: c[q, g, (NC - 1, 0, int(rng.integers(0, NC)))[g % 3], (LEN - 1, 0)[q & 1]] = (int(n[0]) + 1 + int(rng.integers(0, E - 1))) % E
            if m == 2: c[q, g] = n[rng.integers(0, 3, (NC, LEN))]
    return pack(s, x, sq, c)
def check_inputs(d):
    bad = []; a = np.asarray(d["v"]).astype(np.float64)
    if not np.all((np.abs(a) >= 9) & (np.abs(a) <= 23) & (a == np.floor(a))): bad.append("range of v")
    for k in ("sq", "lp"):
        if np.min(d[k]) < 0 or np.max(d[k]) > E - 1: bad.append("range of " + k)
    if not np.all(np.asarray(d["sq"]) == np.asarray(d["sq"])[:1]): bad.append("sq alike on all ranks")
    return bad
def reference(v, sq, lp):
    w = v.astype(np.float32).astype(np.int64).reshape(N, 8, 16, E); tab = sq.astype(np.int64); q = np.arange(N).reshape(N, 1, 1, 1)
    c = np.stack([gentries(a) for a in lp]).astype(np.int64).reshape(N, 8, NC, LEN)
    def pick(names):
        a = np.take_along_axis(w, names.reshape(N, 8, 1, -1), 3); s = np.where(a > 0, 1, -1)
        return s, a - 16 * s
    for rnd in range(RO):
        par = rnd & 1; c = np.roll(c, -par, axis=3); e = c[..., 0::2]; f = c[..., 1::2]; k = f & 7
        f2 = tab[q, k, e]; e2 = tab[q, 8 + k, e]
        se, xe = pick(e); sf, xf = pick(f); sf2, xf2 = pick(f2); se2, xe2 = pick(e2)
        ok = np.all((xe + se * xf == xf2 + sf2 * xe2) & (se * sf == sf2 * se2), axis=2).reshape(e.shape)
        c = np.stack([np.where(ok, f2, e), np.where(ok, e2, f)], axis=4).reshape(N, 8, NC, LEN); c = np.roll(c, par, axis=3)
        c = np.roll(c, DR, axis=0); c[:, :, 1::2] = np.roll(c[:, :, 1::2], DG, axis=1)
    s, x = pick(c); s = s.reshape(N, 8, 16, NC, LEN); x = x.reshape(N, 8, 16, NC, LEN)
    before = np.concatenate([np.ones_like(s[..., :1]), np.multiply.accumulate(s, axis=4)[..., :-1]], axis=4)
    b = np.add.reduce(before * x, axis=4)
    return {"yc": np.stack([gtable(a.reshape(8, -1)) for a in c]).astype(np.float32), "yb": b.reshape(N, 128, NC).astype(np.float32)}

@@ -1,0 +1,291 @@
+from concourse.mybir import AluOpType as ALU, ActivationFunctionType as AF
+
+NQ, C, RO = 4, 32, 5
+WD = 16 * C
+NS = NQ * RO
+BF, H, F, I32, U = "bfloat16", "float16", "float32", "int32", "uint16"
+WTS = (1.0, 61.0, 3728.0, 228352.0)
+MAGIC = 12582912.0
+
+SCRATCH = {
+    "V": ("sbuf", [128, 2048], BF), "Vm": ("sbuf", [128, 2048], BF), "TB": ("sbuf", [128, 16384], BF),
+    "sqi": ("sbuf", [128, 256], I32), "hl": ("sbuf", [128, 512], BF), "stage": ("dram", [4, 16384], BF),
+    "lpi": ("sbuf", [128, 256], I32), "lph": ("sbuf", [128, 256], H),
+    "iot": ("sbuf", [128, 768], BF), "mb": ("sbuf", [128, 1024], BF), "mh": ("sbuf", [128, 1824], H),
+    "tmp": ("sbuf", [128, 256], BF), "zb": ("sbuf", [128, 544], BF),
+    "lnd": ("sbuf", [128, 64 * (NS + NQ)], U), "snd": ("sbuf", [128, 64 * NS], U),
+    "l16": ("sbuf", [128, 64 * (NS + NQ)], H), "q16": ("sbuf", [128, 32 * NS], H), "off": ("sbuf", [128, 32 * NS], U),
+    "pro": ("sbuf", [128, 64 * NS], U), "dl": ("sbuf", [128, 64 * NS], H), "tt": ("sbuf", [128, 64 * NS], H),
+    "ab": ("sbuf", [128, 128 * NS], BF), "okb": ("sbuf", [128, 128 * NS], BF),
+    "wq": ("sbuf", [128, WD * NS], BF), "g1": ("sbuf", [128, WD * NS], BF), "s1": ("sbuf", [128, WD * NS], BF),
+    "p1": ("sbuf", [128, WD * NS], BF), "g2": ("sbuf", [128, WD * NS], BF),
+    "s2": ("sbuf", [128, WD * NS], BF), "p2": ("sbuf", [128, WD * NS], BF),
+    "ycs": ("sbuf", [128, 256], F), "ybs": ("sbuf", [128, 512], F),
+}
+for _b in range(8):
+    SCRATCH["ps%d" % _b] = ("psum", [128, 512], F)
+SEMAPHORES = ["pe", "dve", "act", "pool", "ldq", "ldp", "ldv", "fill", "sta", "stb", "sto", "loc"] + ["ar%d" % i for i in range(NS)]
+
+CY, PCY, GAM, HOP, SELF, DMA_LAT, REM_ISSUE, REM_LAT = 1.0, 0.52, 1.56, 170.0, 110.0, 2200.0, 500.0, 3000.0
+DIGITS = "0123456789abcdefghijklmnopqrstuvwxyzABCDEFGHIJKLMNOPQRSTUVWXYZ"
+ORDER = "0o010300020h0q0m080i06040B0k090n0j0a0E0d0e0f051g0g0D0c1h1i1k1l1n181j1u0A0X0C0z1y1t1m071v0b230p0l1z1w120t0J0v1f1J0s0x0u0r0w0y1A1Z101Y1b191c1a110Z1314161K151o201p0R0S1d17240F0P210I1e0G2u1x2y1B2e1C251G1D1q1r2f1E2t221L1H1M2v1s1I33260K2z1N272w1F1O0H2Z2b2J0Y0O1P2Y2A281Q2x2c1R1S292g301T2d2h1U1V2B1W342i1X2K2C2a2L0L2j352G2k2D310Q2l0M322H2m2E2n0T3e3f2o2M2I2p2q362r0U2F2N2s372O3b3u3t0V2P3v383w2Q3x3c2R2S393g3h2T3d3y2U2V3B2W0N3a3i2X3C3J3j3Z3G3Y3z403k413A3D3l423m3n3H3K3L3E3o433M3I3p3q463r3F3N473s444e3O4t4u4b453P4v483Q4w4c4x3R3S494J4f3T4g4d4h4y3U3V4B3W4i3X4C4j4Y4G4Z4a4z504k0W514A4D4l524m4n4H4K4L4E4o535e4I4M4p4q564r544N4s5f575t4O5u4F5b555v4P584Q5w5c5x4R4S595g5h4T5d4U5y4V5B4W5i4X5J5C5K5j5G5Y5Z5a5z605k615A5D5l625m5n5H5L5E6e5o635M5I5p5q665r5N675s6t6u5O5F646b6v5P6w65685Q6x5R6c5S6f696g5T6d6y5U5V6B5W6a6h6i5X6C6z6D6j6Z6G6Y6A6k706J6l6K716E6H6m726n6L6M6o6I6p6q7e73766r6s6N777f7u6O7t6F7b747v6P7w75786Q7x6R6S7c7g797h6T7d7y6U6V7B6W7a7i7C6X7J7K7Z7j7z7G7Y7k7A807D7l817H7m827n7E7L7M7o7I7p7q83867r7F7s7N8e878f8t7O8u848b8v7P8w85887Q8x7R7S8c8g898h7T8d8y7U7V8B7W8i8C7X8J8K8Y8Z8j8a8z8G908k918A8D8l928m8H8n8L8E8M8o8I9e938p8q968r8F8N978s949f8O9t9b9u958P9v988Q9w9c8R9x8S999g9h8T9d8U8V9y9B8W9a8X9i9J9C9z9j9D9G9Y9Z9A9ka09la19E9H9ma29n9F9K9L9o9I9M9p9qa3a69r9s9Nataeaua79Oa4avabaf9Pawa5a89Qaxac9Raga9ahad9SayaB9Taaai9UaC9VajaZaJaYaG9Wazb09Xakb1aAaDalb2amanaHaKaLaEaFb3aoaIb6apaqb7b4aMbbaNarb8b5asbeaObcaPb9bfbdbgaQbhbzaRaSaTbabibGaUaVbjaWbkbAaXbHbBblbIbCbmbQbJbnbobDbpbXbqbtbYbrbRbsbKbubSbvbwbLbxc7bMbTbNbUc1c8bOc9c2cocac3cbcvcec4cicfcpcwc5cqbEbycjbZbVbFbPc0cgckccbWc6crchcxclcscdcycmctcncu"
+
+
+def build(g, T, send, n_eng):
+    ops = []
+    banks = {}
+    cur = [None, 0]
+    done = []
+
+    def op(eng, fn, cost, deps=(), bank=None, after=(), lat=0.0, sem=None, val=None, far=False):
+        deps = [d for d in deps if d is not None]
+        after = [d for d in after if d is not None]
+        if bank is not None:
+            last = banks.setdefault(bank, {})
+            for e, d in last.items():
+                (after if e == eng else deps).append(d)
+            last[eng] = len(ops)
+        ops.append(dict(tag=cur[0], kind=len(ops) - cur[1], eng=eng, fn=fn, cost=cost, deps=sorted(set(deps)), after=after, lat=lat, sem=sem, val=val, far=far))
+        return len(ops) - 1
+
+    def dve(fn, n, deps, bank=None, half=False, after=()):
+        return op("dve", fn, CY * max(64, n / 2 if half else n) + 10, deps, bank, after)
+
+    def act(fn, n, deps, bank=None):
+        return op("act", fn, CY * max(64, n) + 30, deps, bank)
+
+    def pe(mms, deps, bank, after=()):
+        def fn():
+            for m in mms:
+                ins = g.tensor.matmul(*m[:5])
+            return ins
+        return op("pe", fn, sum(PCY * m[5] + 5 for m in mms), deps, bank, after)
+
+    def dma(eng, out, in_, deps, sem, val, lat):
+        q = g.sync if eng == "sync" else g.scalar
+        return op(eng, lambda: q.dma_start(out, in_), 100.0, deps, lat=lat, sem=sem, val=val)
+
+    def ts(out, in0, a, b, o0, o1=None):
+        if o1 is None:
+            return lambda: g.vector.tensor_scalar(out, in0, a, None, o0)
+        return lambda: g.vector.tensor_scalar(out, in0, a, b, o0, o1)
+
+    def tten(out, in0, in1, o):
+        return lambda: g.vector.tensor_tensor(out, in0, in1, o)
+
+    def cp(out, in_):
+        return lambda: g.vector.tensor_copy(out, in_)
+
+    def mset(ap, c):
+        return lambda: g.vector.memset(ap, c)
+
+    def actf(out, in_, f, **kw):
+        return lambda: g.scalar.activation(out, in_, f, **kw)
+
+    def iota(a, b, pat, base, deps=()):
+        return op("pool", lambda: g.iota(T.iot[:, a:b], pat, base, -1, allow_small_or_imprecise_dtypes=True), 130 + 2 * CY * (b - a), deps)
+
+    lq = dma("sync", T.sqi[:], T.sq[:], [], "ldq", 16, DMA_LAT + 300)
+    lv = dma("act", T.V[:], T.v[:], [], "ldv", 16, DMA_LAT + 1500)
+    lp = dma("sync", T.lpi[:], T.lp[:], [], "ldp", 16, DMA_LAT + 600)
+    m0 = dve(mset(T.TB[:, 0:2048], 0.0), 2048, [], half=True)
+    fills = [m0]
+    fills.append(dma("sync", T.TB[:, 2048:4096], T.TB[:, 0:2048], [m0], "fill", 16, DMA_LAT + 1500))
+    for k in (2, 3):
+        fills.append(act(actf(T.TB[:, 2048 * k:2048 * k + 2048], T.TB[:, 0:2048], AF.Copy), 2048, [m0]))
+    for k in range(8, 14):
+        fills.append(dve(mset(T.TB[:, 1024 * k:1024 * k + 1024], 0.0), 1024, [], half=True))
+    hi = dve(cp(T.hl[:, 0:256], T.sqi[:]), 256, [lq])
+    lo = dve(tten(T.hl[:, 256:512], T.sqi[:], T.hl[:, 0:256], ALU.subtract), 512, [hi])
+    sa = [dma("sync", T.stage[0:2, :], T.hl[:, 0:256], [hi], "sta", 32, DMA_LAT + 600),
+          dma("sync", T.stage[2:4, :], T.hl[:, 256:512], [lo], "sta", 32, DMA_LAT + 600)]
+    iI = iota(0, 128, [[1, 128]], 0)
+    iA = iota(128, 272, [[16, 9], [-1000, 2], [2, 8]], 1000)
+    fills.append(op("pool", lambda: g.iota(T.TB[:, 14336:16384], [[0, 2048]], 0, 0, allow_small_or_imprecise_dtypes=True), 130 + 2 * CY * 2048, after=[iI, iA]))
+    iW = iota(272, 304, [[4, 4], [16, 8]], 0)
+    iX = iota(304, 448, [[4, 9], [-1000, 4], [1, 4]], 3000)
+    iP = [iota(448, 496, [[8, 6], [84, 2], [1, 4]], 0), iota(496, 576, [[8, 10], [-44, 2], [1, 4]], 48)]
+    iB = [iota(576, 600, [[16, 3], [84, 2], [-1, 4]], 3), iota(600, 640, [[16, 5], [-44, 2], [-1, 4]], 51)]
+    iR = iota(640, 768, [[8, 16], [-1, 8]], 7)
+    sb = [dma("sync" if k % 2 == 0 else "act", T.TB[16 * k:16 * k + 4, :], T.stage[:], sa + fills, "stb", 128, DMA_LAT + 2500) for k in range(8)]
+
+    EQ, MUL, ADD, SUB = ALU.is_equal, ALU.mult, ALU.add, ALU.subtract
+    I16, K16, N16 = T.mh[:, 0:128], T.mh[:, 128:256], T.mh[:, 256:384]
+    oI = [dve(ts(I16, T.iot[:, 0:128], 0.0, None, EQ), 128, [iI], half=True),
+          dve(ts(K16, T.iot[:, 0:128], 0.0, 2048.0, EQ, MUL), 128, [iI], half=True),
+          dve(ts(N16, T.iot[:, 0:128], 0.0, -16384.0, EQ, MUL), 128, [iI], half=True),
+          dve(ts(T.mh[:, 1792:1824], T.iot[:, 0:32], 0.0, -1025.0, MUL, ADD), 32, [iI])]
+    CN = T.mh[:, 1792:1824]
+    oA = [dve(ts(T.mh[:, 384 + 144 * t:528 + 144 * t], T.iot[:, 128:272], float(-t), None, EQ), 144, [iA], half=True) for t in range(2)]
+    AM = [[T.mh[:, 384 + 144 * t + 8 * (1 - h):512 + 144 * t + 8 * (1 - h)] for h in range(2)] for t in range(2)]
+    PG, PGP, PGM = T.mh[:, 672:800], T.mh[:, 800:928], T.mh[:, 928:1056]
+    oPG = [dve(ts(PG, T.iot[:, 448:576], 0.0, None, EQ), 128, iP, half=True)]
+    oPP = [dve(ts(T.mh[:, 800 + j:928:4], T.iot[:, 448 + (j + 1) % 4:576:4], 0.0, None, EQ), 32, iP) for j in range(4)]
+    oPM = [dve(ts(T.mh[:, 928 + j:1056:4], T.iot[:, 448 + (j - 1) % 4:576:4], 0.0, None, EQ), 32, iP) for j in range(4)]
+    BM = [[T.mh[:, 1056 + 256 * t + 128 * h:1184 + 256 * t + 128 * h] for h in range(2)] for t in range(2)]
+    oB = []
+    for t in range(2):
+        for h in range(2):
+            a = 1056 + 256 * t + 128 * h
+            oB.append(dve(ts(T.mh[:, a + 1 - t:a + 128:2], T.iot[:, 576:640], float(-8 * h), None, EQ), 64, iB))
+            oB.append(dve(ts(T.mh[:, a + t:a + 128:2], T.iot[:, 576:640], 0.0, None, MUL), 64, iB))
+    REV = T.mh[:, 1568:1696]
+    oR = dve(ts(REV, T.iot[:, 640:768], 0.0, None, EQ), 128, [iR], half=True)
+    IB = T.mb[:, 0:128]
+    oIB = dve(ts(IB, T.iot[:, 0:128], 0.0, None, EQ), 128, [iI], half=True)
+    oX = dve(ts(T.mb[:, 128:272], T.iot[:, 304:448], 0.0, None, EQ), 144, [iX], half=True)
+    w4 = [dve(ts(T.tmp[:, 32 * i:32 * i + 32], T.iot[:, 272:304], float(-i), WTS[i], EQ, MUL), 32, [iW]) for i in range(4)]
+    w2 = dve(tten(T.tmp[:, 128:192], T.tmp[:, 0:64], T.tmp[:, 64:128], ADD), 64, w4)
+    w1 = dve(tten(T.mb[:, 272:304], T.tmp[:, 128:160], T.tmp[:, 160:192], ADD), 64, [w2])
+    oW = [w1] + [dve(ts(T.mb[:, 304 + 32 * i:336 + 32 * i], T.mb[:, 272:304], s, None, MUL), 32, [w1]) for i, s in enumerate((16.0, -1.0, -16.0))]
+    WM = [T.mb[:, 272 + 32 * i:304 + 32 * i] for i in range(4)]
+    oZ = dve(mset(T.zb[:], 0.0), 544, [], half=True)
+    e4 = [dve(ts(T.tmp[:, 192 + 8 * i:200 + 8 * i], T.iot[:, 272:280], float(-i), None, EQ), 8, [iW]) for i in range(4)]
+    oS = [dve(tten(T.zb[:, 128 + 144 * t + 15:128 + 144 * t + 143:16], T.tmp[:, 192 + 8 * t:200 + 8 * t], T.tmp[:, 208 + 8 * t:216 + 8 * t], ADD), 8, e4 + [oZ]) for t in range(2)]
+    ZERO = T.zb[:, 0:128]
+    vm = dve(ts(T.Vm[:], T.V[:], 0.0625, -1.0, MUL, ADD), 2048, [lv], half=True)
+    lh = dve(cp(T.lph[:], T.lpi[:]), 256, [lp])
+
+    ps = [T["ps%d" % b] for b in range(8)]
+    have = []
+    for q in range(NQ):
+        B = 2 * q + 1
+        mm = [pe([(ps[B][:, 320 + 32 * t:352 + 32 * t], AM[t][h], T.lph[:, 64 * q + h:64 * q + 64:2], h == 0, h == 1, 64) for h in range(2)], [lh, oA[t]], B) for t in range(2)]
+        have.append(dve(cp(T.lnd[:, 64 * q:64 * q + 64], ps[B][:, 320:384]), 64, mm, B))
+
+    for r in range(RO):
+        for q in range(NQ):
+            s = r * NQ + q
+            cur[0], cur[1] = s, len(ops)
+            A, B = 2 * q, 2 * q + 1
+            w = slice(WD * s, WD * s + WD)
+            LE, LF = T.lnd[:, 64 * s:64 * s + 32], T.lnd[:, 64 * s + 32:64 * s + 64]
+            HE, HF = T.l16[:, 64 * s:64 * s + 32], T.l16[:, 64 * s + 32:64 * s + 64]
+            got = have[q]
+            d1 = dve(cp(T.l16[:, 64 * s:64 * s + 64], T.lnd[:, 64 * s:64 * s + 64]), 64, [got])
+            Q = T.q16[:, 32 * s:32 * s + 32]
+            d2 = dve(ts(Q, LF, 0.125, 1024.5625, MUL, ADD), 32, [got])
+            o = ps[A][:, 0:32]
+            m1 = pe([(o, K16, HF, True, False, 64), (o, N16, Q, False, False, 64), (o, N16, CN, False, False, 64), (o, I16, HE, False, True, 64)], [d1, d2] + oI, A)
+            OF = T.off[:, 32 * s:32 * s + 32]
+            d3 = dve(cp(OF, o), 32, [m1], A)
+            gq = act(actf(T.wq[:, w], T.TB[:].indirect(OF), AF.Copy), GAM * WD + 35, [d3] + sb)
+            g1 = act(actf(T.g1[:, w], T.V[:].indirect(LE), AF.Copy), GAM * WD + 35, [got, lv])
+            s1 = dve(ts(T.s1[:, w], T.g1[:, w], -1.0, 1.0, ALU.max, ALU.min), WD, [g1], half=True)
+            p1 = dve(tten(T.p1[:, w], T.Vm[:].indirect(LF), T.s1[:, w], MUL), GAM * WD + 40, [s1, vm])
+            m2, d4 = [], []
+            for t in range(2):
+                m2.append(pe([(ps[B][:, 32 * t:32 * t + 32], T.zb[:, 128 + 144 * t + 15 - k:256 + 144 * t + 15 - k], T.wq[:, WD * s + k:WD * s + WD:16], k == 0, k == 15, 64) for k in range(16)],
+                             [gq, oS[t]], B))
+                d4.append(dve(cp(T.pro[:, 64 * s + 32 * t:64 * s + 32 * t + 32], ps[B][:, 32 * t:32 * t + 32]), 32, [m2[t]], B))
+            d5 = dve(tten(T.dl[:, 64 * s:64 * s + 64], ps[B][:, 0:64], T.l16[:, 64 * s:64 * s + 64], SUB), 64, m2 + [d1], B)
+            g2 = act(actf(T.g2[:, w], T.V[:].indirect(T.pro[:, 64 * s:64 * s + 32]), AF.Copy), GAM * WD + 35, [d4[0]])
+            s2 = dve(ts(T.s2[:, w], T.g2[:, w], -1.0, 1.0, ALU.max, ALU.min), WD, [g2], half=True)
+            p2 = dve(tten(T.p2[:, w], T.Vm[:].indirect(T.pro[:, 64 * s + 32:64 * s + 64]), T.s2[:, w], MUL), GAM * WD + 40, [s2, d4[1]])
+            pe([(ps[A][:, 128:256], IB, ZERO, True, False, 128)], [oIB, oZ], A)
+            for i, (buf, dep) in enumerate(((T.g1, g1), (T.p1, p1), (T.g2, g2), (T.p2, p2))):
+                m3 = pe([(ps[A][:, 128 + b:256:4], buf[:, WD * s + b:WD * s + WD:4], WM[i], False, i == 3 and b == 3, 64) for b in range(4)], [dep, oW[i]], A)
+            a1 = act(actf(T.ab[:, 128 * s:128 * s + 128], ps[A][:, 128:256], AF.Abs), 128, [m3], A)
+            m4 = pe([(ps[B][0:32, 128:256], T.ab[:, 128 * s + 32 * k:128 * s + 32 * k + 32], IB, k == 0, k == 3, 128) for k in range(4)], [a1], B)
+            a2 = act(actf(T.okb[0:32, 128 * s:128 * s + 128], ps[B][0:32, 128:256], AF.Relu, bias=1.0, scale=-1.0), 128, [m4], B)
+            m5 = [pe([(ps[B][:, 256 + 32 * t:288 + 32 * t], T.mb[0:32, 140 - 4 * a:268 - 4 * a], T.okb[0:32, 128 * s + a:128 * s + 128:4], a == 0, a == 3, 64) for a in range(4)],
+                     [a2, oX], B) for t in range(2)]
+            d6 = dve(tten(T.tt[:, 64 * s:64 * s + 64], ps[B][:, 256:320], T.dl[:, 64 * s:64 * s + 64], MUL), 64, m5 + [d5], B)
+            TE, TF = T.tt[:, 64 * s:64 * s + 32], T.tt[:, 64 * s + 32:64 * s + 64]
+            if r < RO - 1:
+                ME, MF, dm = (PG, PGP, oPG + oPP) if r % 2 == 0 else (PGM, PG, oPG + oPM)
+                oE, oF = ps[B][:, 320:352], ps[B][:, 352:384]
+                m6 = [pe([(oE, ME, HF, True, False, 64), (oE, ME, TF, False, True, 64)], [d6] + dm, B),
+                      pe([(oF, MF, HE, True, False, 64), (oF, MF, TE, False, True, 64)], [d6] + dm, B)]
+            else:
+                m6 = [pe([(ps[B][:, 320 + h:384:2], BM[0][h], HE, True, False, 64), (ps[B][:, 320 + h:384:2], BM[1][h], HF, False, False, 64),
+                          (ps[B][:, 320 + h:384:2], BM[0][h], TE, False, False, 64), (ps[B][:, 320 + h:384:2], BM[1][h], TF, False, True, 64)], [d6] + oB, B) for h in range(2)]
+            d7 = dve(cp(T.snd[:, 64 * s:64 * s + 64], ps[B][:, 320:384]), 64, m6, B)
+            done.append(d7)
+            have[q] = op("pool", send(T.lnd[:, 64 * (s + NQ):64 * (s + NQ) + 64], T.snd[:, 64 * s:64 * s + 64], "ar%d" % s), REM_ISSUE, [d7],
+                         lat=REM_LAT, sem="ar%d" % s, val=n_eng, far=True)
+
+    n_st = 2 * NQ
+    for q in range(NQ):
+        s = NS + q
+        cur[0], cur[1] = s, len(ops)
+        B = 2 * q + 1
+        got = have[q]
+        outs = []
+        FG, FS, FZ = T.wq, T.g1, T.s1
+        for u in range(2):
+            a = 1024 * q + 512 * u
+            fg = act(actf(FG[:, a:a + 512], T.Vm[:].indirect(T.lnd[:, 64 * s + 32 * u:64 * s + 32 * u + 32]), AF.Copy), GAM * 512 + 35, [got, done[a // WD]])
+            fs = dve(ts(FS[:, a:a + 512], FG[:, a:a + 512], MAGIC + 1.0, MAGIC, ADD, SUB), 512, [fg], half=True)
+            fx = dve(tten(FG[:, a:a + 512:8], FG[:, a:a + 512:8], FS[:, a:a + 512:8], SUB), 128, [fs])
+            f0 = dve(mset(FS[:, a:a + 512:8], 0.0), 64, [fx])
+            sc = dve(lambda a=a: g.vector.tensor_tensor_scan(FZ[:, a:a + 512], FS[:, a:a + 512], FG[:, a:a + 512], 0.0, MUL, ADD), 512, [f0], half=True)
+            outs.append(act(actf(T.ybs[:, a // 8:a // 8 + 64], FZ[:, a + 7:a + 512:8], AF.Identity, bias=16.0, scale=16.0), 64, [sc]))
+        dma("sync", T.yb[:, 128 * q:128 * q + 128], T.ybs[:, 128 * q:128 * q + 128], outs, "sto", 16 * n_st, DMA_LAT)
+        d1 = dve(cp(T.l16[:, 64 * s:64 * s + 64], T.lnd[:, 64 * s:64 * s + 64]), 64, [got])
+        m = pe([(ps[B][:, 384:448], REV, T.l16[:, 64 * s:64 * s + 64], True, True, 64)], [d1, oR], B)
+        c = act(actf(T.ycs[:, 64 * q:64 * q + 64], ps[B][:, 384:448], AF.Copy), 64, [m], B)
+        dma("sync", T.yc[:, 64 * q:64 * q + 64], T.ycs[:, 64 * q:64 * q + 64], [c], "sto", 16 * n_st, DMA_LAT)
+    return ops
+
+
+def schedule(ops):
+    order = [62 * DIGITS.index(ORDER[k]) + DIGITS.index(ORDER[k + 1]) for k in range(0, len(ORDER), 2)]
+    place = {i: k for k, i in enumerate(order)}
+    assert len(place) == len(ops) and all(place[d] < place[i] for i, o in enumerate(ops) for d in o["deps"] + o["after"])
+    return order
+
+
+def emit(g, T, ops, order):
+    queue = {"pe": g.tensor, "dve": g.vector, "act": g.scalar, "pool": g, "sync": g.sync}
+    count = {"pe": 0, "dve": 0, "act": 0, "pool": 0}
+    seen = {e: {} for e in queue}
+    clock = {}
+    total = {}
+    for i in order:
+        o = ops[i]
+        e = o["eng"]
+        need = {}
+        for d in o["deps"]:
+            s, v = ops[d]["sem"], ops[d]["val"]
+            if v > need.get(s, (0, None))[0]:
+                need[s] = (v, d)
+        for s, (v, d) in sorted(need.items(), key=lambda x: -x[1][1]):
+            if seen[e].get(s, 0) < v:
+                queue[e].wait_ge(T.sem[s], v)
+                seen[e][s] = v
+                if not ops[d]["far"]:
+                    for s2, v2 in clock[d].items():
+                        seen[e][s2] = max(seen[e].get(s2, 0), v2)
+        ins = o["fn"]()
+        clock[i] = dict(seen[e])
+        if o["sem"] is None:
+            count[e] += 1
+            o["sem"], o["val"] = e, count[e]
+            ins.then_inc(T.sem[e], 1)
+        elif not o["far"]:
+            ins.then_inc(T.sem[o["sem"]], 16)
+        total[o["sem"]] = max(total.get(o["sem"], 0), o["val"])
+    return total, seen
+
+
+def rank_program(g, core, T, topo):
+    rank = T.rank_of(core)
+    if rank is None:
+        return
+    nxt = T.cores[(rank + 1) % len(T.cores)]
+    prv = T.cores[(rank - 1) % len(T.cores)]
+    assert topo.may_write(core, nxt)
+    rid, pid = topo.addr(nxt)[:2]
+    mask = topo.mask(core, nxt)
+
+    def send(out, in_, sem):
+        return lambda: g.remote_dma(out, in_, T.sem[sem], T.sem.loc, pid, rid, mask)
+
+    ops = build(g, T, send, len(topo.engines(prv, core)))
+    order = schedule(ops)
+    total, seen = emit(g, T, ops, order)
+    total["loc"] = NS * len(topo.engines(core, nxt))
+    for s, v in total.items():
+        if all(seen[e].get(s, 0) < v for e in seen):
+            g.wait_ge(T.sem[s], v)

@@ -1,43 +1,62 @@
 from concourse.mybir import AluOpType as ALU, ActivationFunctionType as AF
 
-NQ, C, RO = 4, 32, 5
-WD = 16 * C
+RO = 5
+CS = (32, 32, 32, 32)
+NQ = len(CS)
+LO = [sum(CS[:q]) for q in range(NQ)]
 NS = NQ * RO
 BF, H, F, I32, U = "bfloat16", "float16", "float32", "int32", "uint16"
 WTS = (1.0, 61.0, 3728.0, 228352.0)
 MAGIC = 12582912.0
+LW = 128 * RO
 
 SCRATCH = {
     "V": ("sbuf", [128, 2048], BF), "Vm": ("sbuf", [128, 2048], BF), "TB": ("sbuf", [128, 16384], BF),
     "sqi": ("sbuf", [128, 256], I32), "hl": ("sbuf", [128, 512], BF), "stage": ("dram", [4, 16384], BF),
-    "lpi": ("sbuf", [128, 256], I32), "lph": ("sbuf", [128, 256], H),
-    "iot": ("sbuf", [128, 768], BF), "mb": ("sbuf", [128, 1024], BF), "mh": ("sbuf", [128, 1824], H),
-    "tmp": ("sbuf", [128, 256], BF), "zb": ("sbuf", [128, 544], BF),
-    "lnd": ("sbuf", [128, 64 * (NS + NQ)], U), "snd": ("sbuf", [128, 64 * NS], U),
-    "l16": ("sbuf", [128, 64 * (NS + NQ)], H), "q16": ("sbuf", [128, 32 * NS], H), "off": ("sbuf", [128, 32 * NS], U),
-    "pro": ("sbuf", [128, 64 * NS], U), "dl": ("sbuf", [128, 64 * NS], H), "tt": ("sbuf", [128, 64 * NS], H),
-    "ab": ("sbuf", [128, 128 * NS], BF), "okb": ("sbuf", [128, 128 * NS], BF),
-    "wq": ("sbuf", [128, WD * NS], BF), "g1": ("sbuf", [128, WD * NS], BF), "s1": ("sbuf", [128, WD * NS], BF),
-    "p1": ("sbuf", [128, WD * NS], BF), "g2": ("sbuf", [128, WD * NS], BF),
-    "s2": ("sbuf", [128, WD * NS], BF), "p2": ("sbuf", [128, WD * NS], BF),
+    "lpi": ("sbuf", [128, 256], I32), "lph": ("sbuf", [128, 256], H), "lpq": ("sbuf", [128, 256], H),
+    "zb": ("sbuf", [128, 1184], BF), "mt": ("sbuf", [128, 2080], H),
+    "lnd": ("sbuf", [128, 2 * LW], H), "snd": ("sbuf", [128, 2 * LW], H), "neg": ("sbuf", [128, 2 * LW], H),
+    "lst": ("sbuf", [128, 5 * LW + 256], U),
+    "l16": ("sbuf", [128, 4 * LW], H), "q8": ("sbuf", [128, LW], H), "e16": ("sbuf", [128, LW], H),
+    "ab": ("sbuf", [128, 4 * LW], BF),
     "ycs": ("sbuf", [128, 256], F), "ybs": ("sbuf", [128, 512], F),
 }
+for _n in ("wq", "g1", "s1", "p1", "g2", "s2", "p2"):
+    SCRATCH[_n] = ("sbuf", [128, 16 * LW], BF)
 for _b in range(8):
     SCRATCH["ps%d" % _b] = ("psum", [128, 512], F)
 SEMAPHORES = ["pe", "dve", "act", "pool", "ldq", "ldp", "ldv", "fill", "sta", "stb", "sto", "loc"] + ["ar%d" % i for i in range(NS)]
 
-CY, PCY, GAM, HOP, SELF, DMA_LAT, REM_ISSUE, REM_LAT = 1.0, 0.52, 1.56, 170.0, 110.0, 2200.0, 500.0, 3000.0
-DIGITS = "0123456789abcdefghijklmnopqrstuvwxyzABCDEFGHIJKLMNOPQRSTUVWXYZ"
-ORDER = "0o010300020h0q0m080i06040B0k090n0j0a0E0d0e0f051g0g0D0c1h1i1k1l1n181j1u0A0X0C0z1y1t1m071v0b230p0l1z1w120t0J0v1f1J0s0x0u0r0w0y1A1Z101Y1b191c1a110Z1314161K151o201p0R0S1d17240F0P210I1e0G2u1x2y1B2e1C251G1D1q1r2f1E2t221L1H1M2v1s1I33260K2z1N272w1F1O0H2Z2b2J0Y0O1P2Y2A281Q2x2c1R1S292g301T2d2h1U1V2B1W342i1X2K2C2a2L0L2j352G2k2D310Q2l0M322H2m2E2n0T3e3f2o2M2I2p2q362r0U2F2N2s372O3b3u3t0V2P3v383w2Q3x3c2R2S393g3h2T3d3y2U2V3B2W0N3a3i2X3C3J3j3Z3G3Y3z403k413A3D3l423m3n3H3K3L3E3o433M3I3p3q463r3F3N473s444e3O4t4u4b453P4v483Q4w4c4x3R3S494J4f3T4g4d4h4y3U3V4B3W4i3X4C4j4Y4G4Z4a4z504k0W514A4D4l524m4n4H4K4L4E4o535e4I4M4p4q564r544N4s5f575t4O5u4F5b555v4P584Q5w5c5x4R4S595g5h4T5d4U5y4V5B4W5i4X5J5C5K5j5G5Y5Z5a5z605k615A5D5l625m5n5H5L5E6e5o635M5I5p5q665r5N675s6t6u5O5F646b6v5P6w65685Q6x5R6c5S6f696g5T6d6y5U5V6B5W6a6h6i5X6C6z6D6j6Z6G6Y6A6k706J6l6K716E6H6m726n6L6M6o6I6p6q7e73766r6s6N777f7u6O7t6F7b747v6P7w75786Q7x6R6S7c7g797h6T7d7y6U6V7B6W7a7i7C6X7J7K7Z7j7z7G7Y7k7A807D7l817H7m827n7E7L7M7o7I7p7q83867r7F7s7N8e878f8t7O8u848b8v7P8w85887Q8x7R7S8c8g898h7T8d8y7U7V8B7W8i8C7X8J8K8Y8Z8j8a8z8G908k918A8D8l928m8H8n8L8E8M8o8I9e938p8q968r8F8N978s949f8O9t9b9u958P9v988Q9w9c8R9x8S999g9h8T9d8U8V9y9B8W9a8X9i9J9C9z9j9D9G9Y9Z9A9ka09la19E9H9ma29n9F9K9L9o9I9M9p9qa3a69r9s9Nataeaua79Oa4avabaf9Pawa5a89Qaxac9Raga9ahad9SayaB9Taaai9UaC9VajaZaJaYaG9Wazb09Xakb1aAaDalb2amanaHaKaLaEaFb3aoaIb6apaqb7b4aMbbaNarb8b5asbeaObcaPb9bfbdbgaQbhbzaRaSaTbabibGaUaVbjaWbkbAaXbHbBblbIbCbmbQbJbnbobDbpbXbqbtbYbrbRbsbKbubSbvbwbLbxc7bMbTbNbUc1c8bOc9c2cocac3cbcvcec4cicfcpcwc5cqbEbycjbZbVbFbPc0cgckccbWc6crchcxclcscdcycmctcncu"
+OPT = dict(split=0, d40="dve", stc=(3,), stb=(1, 2, 3), fgd=(3,), half=(3,), sa=0, pack=0, foq="act", ta=2, f0=4, fd=9, fa=3, fp=2, vm="act", okq="act", absq="act")
+
+TIME = dict(d2=-0.326, dn=-0.321, m1=-0.316, d3=0.114, gq=0.12, g1=0.125, s1=0.683, sa=0.7, p1=1.118, m2=0.681, d40=0.682, d5=1.688, dx=0.95, mx=0.689, d41=1.144, mo=1.962,
+            g2=1.049, s2=1.148, p2=1.41, m30=1.68, m31=1.68, m32=1.684, m33=1.688, a1=2.061, m5=2.062, d6=2.229, send=2.3, late=2.4,
+            yn=-0.32, yr=-0.307, ym=0.684, yl=0.127, yo=1.03, st=1.1, fg0=0.13, fg1=0.14, fs0=1.127, fs1=1.13, fx0=1.13, fx1=1.424, fz0=1.23, fz1=1.683, sc0=1.674, sc1=2.13, fo0=2.2, fo1=2.3, sb=2.4)
+EARLY = dict(m1=-3.0, d3=-2.9, g1=-2.0, s1=-1.9, p1=-1.85, gap=0.1)
+FIRST = dict(gq=-0.731, m2=-0.124, d40=0.311, mx=0.716, d41=0.72, d5=0.73, mo=1.24, g2=0.312, s2=0.736, p2=1.49, m30=1.206, m31=1.568, m32=1.751, m33=1.752,
+             a1=1.981, m5=2.129, d6=2.43, send=2.44, late=3.212, step=0.958)
+ONCE = dict(zero=-30.0, load=-34.0, filld=-25.0, fille=-6.0, filla=-12.0, hi=-10.0, vm=-9.0, lh=-8.0, l8=-2.95, stage=-5.0, table=-4.0, tabla=-4.0, ma0=-20.0, fillp=-19.0, mat=-18.0, wm=-1.0)
+OPT.update(stc=(1, 3), stb=(0, 1, 2, 3), fgd=(), half=(0, 1, 2, 3))
+TIME.update(yr=-0.4416, m1=-0.4376, d2=-0.416, dn=-0.1843, yn=-0.1767, fg0=0.0468, d3=0.0584, yl=0.0637, gq=0.0646, ym=0.3613, m2=0.3749, g1=0.3764, sa=0.7, d40=0.8385, fs0=0.8477, s1=0.851, mx=0.8863, g2=0.9177, fg1=0.9239, yo=0.9367, dx=0.95, m30=1.0038, m31=1.0207, p1=1.0698, fx0=1.1437, fs1=1.1581, fz0=1.1655, s2=1.2891, d41=1.3035, send=1.4138, fx1=1.5557, m32=1.6654, sc0=1.8069, fz1=1.8104, p2=1.8347, m33=1.869, d5=1.9677, mo=2.0111, m5=2.0148, a1=2.0282, sc1=2.0607, late=2.4, d6=2.4948, st=3.0174, fo0=4.9958, fo1=5.501, sb=8.4394)
+FIRST.update(m2=-2.5643, gq=-2.3448, late=0.3, d40=-1.3664, mx=-0.8627, d41=-0.2159, g2=-0.1188, send=0.169, m30=0.2583, m31=0.4495, m32=0.6463, s2=0.663, m33=0.7454, p2=0.7533, d5=0.8701, mo=1.0644, step=1.1066, a1=1.1693, m5=1.3099, d6=1.7768)
+EARLY.update(g1=-3.4012, m1=-2.6935, d3=-2.317, s1=-1.7403, p1=-1.1938, gap=-0.3188)
+ONCE.update(load=-33.9596, stage=-33.9532, table=-33.951, filld=-24.5007, zero=-24.6, hi=-24.3489, fille=-21.6925, lh=-21.6898, l8=-21.6454, fillp=-18.3, ma0=-18.3914, mat=-18.2, filla=-10.8913, vm=-10.7232, tabla=-10.7145, wm=-0.5164)
+TIME.update(m1=-0.4376, d2=-0.416, yr=-0.3137, yn=-0.221, dn=-0.1843, yl=0.0072, d3=0.0584, gq=0.0646, fg0=0.3473, ym=0.3625, fg1=0.3638, m2=0.3749, g1=0.3764, sa=0.7, d40=0.8385, s1=0.851, mx=0.8863, g2=0.9177, yo=0.9411, dx=0.95, fs0=0.9659, m30=1.0038, fx0=1.0195, m31=1.0207, fs1=1.0299, p1=1.0698, fz0=1.2422, s2=1.2891, d41=1.3035, send=1.4138, fx1=1.5092, m32=1.6654, sc0=1.7269, fz1=1.7424, p2=1.8347, m33=1.869, fo0=1.9466, fo1=1.9501, d5=1.9677, sc1=1.9716, mo=2.0111, m5=2.0148, a1=2.0282, late=2.4, d6=2.4948, st=5.5666, sb=6.5788)
+FIRST.update(m30=-2.6426, m2=-1.2616, d40=-0.7226, gq=-0.6722, mx=-0.4486, send=-0.0151, d41=0.2488, s2=0.2624, late=0.3, g2=0.4073, m31=0.54, m32=0.701, m33=0.7173, step=1.0749, mo=1.1182, p2=1.2391, d5=1.2473, m5=1.4121, a1=1.4863, d6=1.8753)
+EARLY.update(m1=-4.8904, d3=-3.9577, g1=-0.813, s1=-0.7792, p1=-0.7624, gap=0.0179)
+ONCE.update(load=-38, stage=-37, table=-36, zero=-30, filld=-29, hi=-28, lh=-27, l8=-25, fille=-26, wm=-1, fillp=-17, ma0=-18, mat=-16, filla=-3, vm=-2, tabla=-1)
+FIRST.update(gq=-2.0633, m2=-1.8185, mx=-0.7396, d40=-0.7041, d41=-0.1993, s2=-0.1932, g2=0.1252, m30=0.3332, send=0.3425, m31=0.3449, late=0.35, m32=0.3513, m33=0.3717, p2=0.8851, d5=0.9001, step=1.107, mo=1.1187, a1=1.2393, m5=1.3245, d6=1.7964)
+EARLY.update(d3=-8.6204, g1=-3.2076, m1=-2.2665, s1=-0.8843, p1=-0.8287, gap=0.044)
+ONCE.update(load=-37.3197, stage=-37.1808, table=-37.163, filld=-28.8134, hi=-28.5992, zero=-28.2568, fille=-28.2541, lh=-28.2222, l8=-28.2056, fillp=-18.1182, ma0=-18.1126, mat=-18.1094, filla=-4.1238, vm=-4.1155, tabla=-4.097, wm=-0.75)
 
 
 def build(g, T, send, n_eng):
     ops = []
     banks = {}
-    cur = [None, 0]
-    done = []
+    done = {}
+    cur = [None]
 
-    def op(eng, fn, cost, deps=(), bank=None, after=(), lat=0.0, sem=None, val=None, far=False):
+    def op(eng, name, fn, deps=(), bank=None, after=(), sem=None, val=None, far=False):
         deps = [d for d in deps if d is not None]
         after = [d for d in after if d is not None]
         if bank is not None:
@@ -45,194 +64,280 @@ def build(g, T, send, n_eng):
             for e, d in last.items():
                 (after if e == eng else deps).append(d)
             last[eng] = len(ops)
-        ops.append(dict(tag=cur[0], kind=len(ops) - cur[1], eng=eng, fn=fn, cost=cost, deps=sorted(set(deps)), after=after, lat=lat, sem=sem, val=val, far=far))
+        ops.append(dict(beat=cur[0], name=name, eng=eng, fn=fn, deps=sorted(set(deps)), after=after, sem=sem, val=val, far=far))
         return len(ops) - 1
 
-    def dve(fn, n, deps, bank=None, half=False, after=()):
-        return op("dve", fn, CY * max(64, n / 2 if half else n) + 10, deps, bank, after)
-
-    def act(fn, n, deps, bank=None):
-        return op("act", fn, CY * max(64, n) + 30, deps, bank)
-
-    def pe(mms, deps, bank, after=()):
+    def pe(name, mms, deps, bank):
         def fn():
             for m in mms:
-                ins = g.tensor.matmul(*m[:5])
+                ins = g.tensor.matmul(*m)
             return ins
-        return op("pe", fn, sum(PCY * m[5] + 5 for m in mms), deps, bank, after)
+        return op("pe", name, fn, deps, bank)
 
-    def dma(eng, out, in_, deps, sem, val, lat):
+    def dma(eng, name, out, in_, deps, sem, val):
         q = g.sync if eng == "sync" else g.scalar
-        return op(eng, lambda: q.dma_start(out, in_), 100.0, deps, lat=lat, sem=sem, val=val)
+        return op(eng, name, lambda: q.dma_start(out, in_), deps, sem=sem, val=val)
 
-    def ts(out, in0, a, b, o0, o1=None):
+    def ts(name, out, in0, a, b, o0, o1, deps, bank=None):
         if o1 is None:
-            return lambda: g.vector.tensor_scalar(out, in0, a, None, o0)
-        return lambda: g.vector.tensor_scalar(out, in0, a, b, o0, o1)
+            return op("dve", name, lambda: g.vector.tensor_scalar(out, in0, a, None, o0), deps, bank)
+        return op("dve", name, lambda: g.vector.tensor_scalar(out, in0, a, b, o0, o1), deps, bank)
 
-    def tten(out, in0, in1, o):
-        return lambda: g.vector.tensor_tensor(out, in0, in1, o)
+    def tten(name, out, in0, in1, o, deps, bank=None):
+        return op("dve", name, lambda: g.vector.tensor_tensor(out, in0, in1, o), deps, bank)
 
-    def cp(out, in_):
-        return lambda: g.vector.tensor_copy(out, in_)
+    def cp(name, out, in_, deps, bank=None):
+        return op("dve", name, lambda: g.vector.tensor_copy(out, in_), deps, bank)
 
-    def mset(ap, c):
-        return lambda: g.vector.memset(ap, c)
+    def mset(name, ap, c, deps=()):
+        return op("dve", name, lambda: g.vector.memset(ap, c), deps)
 
-    def actf(out, in_, f, **kw):
-        return lambda: g.scalar.activation(out, in_, f, **kw)
-
-    def iota(a, b, pat, base, deps=()):
-        return op("pool", lambda: g.iota(T.iot[:, a:b], pat, base, -1, allow_small_or_imprecise_dtypes=True), 130 + 2 * CY * (b - a), deps)
-
-    lq = dma("sync", T.sqi[:], T.sq[:], [], "ldq", 16, DMA_LAT + 300)
-    lv = dma("act", T.V[:], T.v[:], [], "ldv", 16, DMA_LAT + 1500)
-    lp = dma("sync", T.lpi[:], T.lp[:], [], "ldp", 16, DMA_LAT + 600)
-    m0 = dve(mset(T.TB[:, 0:2048], 0.0), 2048, [], half=True)
-    fills = [m0]
-    fills.append(dma("sync", T.TB[:, 2048:4096], T.TB[:, 0:2048], [m0], "fill", 16, DMA_LAT + 1500))
-    for k in (2, 3):
-        fills.append(act(actf(T.TB[:, 2048 * k:2048 * k + 2048], T.TB[:, 0:2048], AF.Copy), 2048, [m0]))
-    for k in range(8, 14):
-        fills.append(dve(mset(T.TB[:, 1024 * k:1024 * k + 1024], 0.0), 1024, [], half=True))
-    hi = dve(cp(T.hl[:, 0:256], T.sqi[:]), 256, [lq])
-    lo = dve(tten(T.hl[:, 256:512], T.sqi[:], T.hl[:, 0:256], ALU.subtract), 512, [hi])
-    sa = [dma("sync", T.stage[0:2, :], T.hl[:, 0:256], [hi], "sta", 32, DMA_LAT + 600),
-          dma("sync", T.stage[2:4, :], T.hl[:, 256:512], [lo], "sta", 32, DMA_LAT + 600)]
-    iI = iota(0, 128, [[1, 128]], 0)
-    iA = iota(128, 272, [[16, 9], [-1000, 2], [2, 8]], 1000)
-    fills.append(op("pool", lambda: g.iota(T.TB[:, 14336:16384], [[0, 2048]], 0, 0, allow_small_or_imprecise_dtypes=True), 130 + 2 * CY * 2048, after=[iI, iA]))
-    iW = iota(272, 304, [[4, 4], [16, 8]], 0)
-    iX = iota(304, 448, [[4, 9], [-1000, 4], [1, 4]], 3000)
-    iP = [iota(448, 496, [[8, 6], [84, 2], [1, 4]], 0), iota(496, 576, [[8, 10], [-44, 2], [1, 4]], 48)]
-    iB = [iota(576, 600, [[16, 3], [84, 2], [-1, 4]], 3), iota(600, 640, [[16, 5], [-44, 2], [-1, 4]], 51)]
-    iR = iota(640, 768, [[8, 16], [-1, 8]], 7)
-    sb = [dma("sync" if k % 2 == 0 else "act", T.TB[16 * k:16 * k + 4, :], T.stage[:], sa + fills, "stb", 128, DMA_LAT + 2500) for k in range(8)]
+    def act(name, out, in_, f, deps, bank=None, **kw):
+        return op("act", name, lambda: g.scalar.activation(out, in_, f, **kw), deps, bank)
 
     EQ, MUL, ADD, SUB = ALU.is_equal, ALU.mult, ALU.add, ALU.subtract
-    I16, K16, N16 = T.mh[:, 0:128], T.mh[:, 128:256], T.mh[:, 256:384]
-    oI = [dve(ts(I16, T.iot[:, 0:128], 0.0, None, EQ), 128, [iI], half=True),
-          dve(ts(K16, T.iot[:, 0:128], 0.0, 2048.0, EQ, MUL), 128, [iI], half=True),
-          dve(ts(N16, T.iot[:, 0:128], 0.0, -16384.0, EQ, MUL), 128, [iI], half=True),
-          dve(ts(T.mh[:, 1792:1824], T.iot[:, 0:32], 0.0, -1025.0, MUL, ADD), 32, [iI])]
-    CN = T.mh[:, 1792:1824]
-    oA = [dve(ts(T.mh[:, 384 + 144 * t:528 + 144 * t], T.iot[:, 128:272], float(-t), None, EQ), 144, [iA], half=True) for t in range(2)]
-    AM = [[T.mh[:, 384 + 144 * t + 8 * (1 - h):512 + 144 * t + 8 * (1 - h)] for h in range(2)] for t in range(2)]
-    PG, PGP, PGM = T.mh[:, 672:800], T.mh[:, 800:928], T.mh[:, 928:1056]
-    oPG = [dve(ts(PG, T.iot[:, 448:576], 0.0, None, EQ), 128, iP, half=True)]
-    oPP = [dve(ts(T.mh[:, 800 + j:928:4], T.iot[:, 448 + (j + 1) % 4:576:4], 0.0, None, EQ), 32, iP) for j in range(4)]
-    oPM = [dve(ts(T.mh[:, 928 + j:1056:4], T.iot[:, 448 + (j - 1) % 4:576:4], 0.0, None, EQ), 32, iP) for j in range(4)]
-    BM = [[T.mh[:, 1056 + 256 * t + 128 * h:1184 + 256 * t + 128 * h] for h in range(2)] for t in range(2)]
+
+    def sel(name, out, in_, pat, cmp, fill, base, cm, deps):
+        return op("pool", name, lambda: g.affine_select(out, in_, pat, cmp, fill, base, cm), deps)
+
+    def mark(name, out, in_, pat, base, c, deps):
+        return sel(name, out, in_, pat, ALU.not_equal, c, base, -1, deps)
+
+    def copy(name, out, in_, n, deps):
+        return sel(name, out, in_, [[0, n]], ALU.is_ge, 0.0, 0, 0, deps)
+
+    lq = dma("sync", "load", T.sqi[:], T.sq[:], [], "ldq", 16)
+    lp = dma("sync", "load", T.lpi[:], T.lp[:], [], "ldp", 16)
+    oZ = mset("zero", T.zb[:], 0.0)
+    lv = dma("act", "load", T.V[:], T.v[:], [], "ldv", 16)
+    nd, na = OPT["fd"], OPT["fa"]
+    fills = [mset("filld" if k < OPT["f0"] else "fille", T.TB[:, 1024 * k:1024 * k + 1024], 0.0) for k in range(nd)]
+    afill = [act("filla", T.TB[:, 1024 * k:1024 * k + 1024], T.TB[:, 0:1024], AF.Copy, fills[:1]) for k in range(nd, nd + na)]
+    fills += afill
+    nf = nd + na + OPT["fp"]
+    if OPT["fp"]:
+        fills.append(op("pool", "fillp", lambda: g.iota(T.TB[:, 1024 * (nd + na):1024 * nf], [[0, 1024 * OPT["fp"]]], 0, 0, allow_small_or_imprecise_dtypes=True)))
+    for k in range(nf // 2, 8):
+        fills.append(dma("sync", "load", T.TB[:, 2048 * k:2048 * k + 2048], T.v[:], [], "fill", 16 * (8 - nf // 2)))
+    hi = cp("hi", T.hl[:, 0:256], T.sqi[:], [lq])
+    lo = tten("hi", T.hl[:, 256:512], T.sqi[:], T.hl[:, 0:256], SUB, [hi])
+    sa = [dma("sync", "stage", T.stage[0:2, :], T.hl[:, 0:256], [hi], "sta", 32),
+          dma("sync", "stage", T.stage[2:4, :], T.hl[:, 256:512], [lo], "sta", 32)]
+    sb = [dma("act" if k < OPT["ta"] else "sync", "tabla" if k < OPT["ta"] else "table", T.TB[16 * k:16 * k + 4, :], T.stage[:], sa + fills, "stb", 128) for k in range(8)]
+
+    Z = T.zb
+    ZERO = Z[:, 0:128]
+    M = T.mt
+    AM, oA = [], []
+    for i, (t, c) in enumerate(((1, 2048.0), (0, 1.0), (1, 1.0))):
+        oA.append(mark("ma0", M[:, 144 * i:144 * i + 144], Z[:, 0:144], [[16, 9], [-1000, 2], [2, 8]], 1000 + t, c, [oZ]))
+        AM.append([M[:, 144 * i + 8 * (1 - h):144 * i + 128 + 8 * (1 - h)] for h in range(2)])
+    oC = [sel("mat" if i else "ma0", M[:, 432 + 64 * i:496 + 64 * i], Z[:, 0:64], [[0, 64]], ALU.is_gt, c, 0, 0, [oZ]) for i, c in enumerate((12288.0, 1.0, 2048.0))]
+    NK, PI = M[:, 624:752], M[:, 752:880]
+    w0 = 432 + 96
+    XP = [[-4, 9], [1000, 4], [-32, 4]]
+    oS = oW = oX = oZ
+    oI = []
+    for i in range(4):
+        oW = mark("mat", Z[:, w0:w0 + 32], Z[:, w0:w0 + 32], [[16, 8], [4, 4]], i, WTS[i], [oW])
+        col = Z[:, 303:431:16] if OPT["pack"] == 1 or i % 2 == 0 else Z[:, 1055:1183:16]
+        oS = mark("mat", col, col, [[16, 8]], i, (1.0, 1 / 2048)[i % 2] if OPT["pack"] == 1 else 1.0, [oS])
+        if i % 2 == 0:
+            oI.append(mark("mat", (NK, PI)[i // 2], ZERO, [[1, 128]], 0, (-2048.0, 1.0)[i // 2], [oZ]))
+        else:
+            oX = sel("mat", Z[:, 144:288], Z[:, 144:288], XP, ALU.is_ge, (-4096.0, 0.0)[i // 2], 4 * (i // 2), 1, [oX])
+    oW = [oW] + [ts("wm", Z[:, w0 + 128 * i:w0 + 128 * i + 32], Z[:, w0:w0 + 32], c, None, MUL, None, [oW]) for i, c in ((1, 16.0), (2, -1.0), (3, -16.0))]
+    WM = [[Z[:, w0 + 128 * i - 32 * a:w0 + 128 * i - 32 * a + 128] for a in range(4)] for i in range(4)]
+    XM = [Z[:, 160 - 4 * b:288 - 4 * b] for b in range(4)]
+    PG, KG, PGP, KP, PGM = (M[:, a:a + 128] for a in (880, 1008, 1136, 1264, 1392))
+    oPG = [mark("mat", M[:, m + a:m + a + n], Z[:, 0:n], [[8, n // 8], [st, 2], [1, 4]], a, c, [oZ])
+           for m, c in ((880, 1.0), (1008, 2048.0)) for a, n, st in ((0, 48, 84), (48, 80, -44))]
+    z = [copy("mat", M[:, m + 256:m + 383], M[:, m + 1:m + 128], 127, oPG) for m in (880, 1008)]
+    oPP = [copy("mat", M[:, m + 259:m + 384:4], M[:, m:m + 128:4], 32, z) for m in (880, 1008)]
+    cur[0] = 0
+    z = copy("late", M[:, 1393:1520], M[:, 880:1007], 127, oPG)
+    cur[0] = 1
+    oPM = [copy("late", M[:, 1392:1520:4], M[:, 883:1008:4], 32, [z])]
     oB = []
-    for t in range(2):
-        for h in range(2):
-            a = 1056 + 256 * t + 128 * h
-            oB.append(dve(ts(T.mh[:, a + 1 - t:a + 128:2], T.iot[:, 576:640], float(-8 * h), None, EQ), 64, iB))
-            oB.append(dve(ts(T.mh[:, a + t:a + 128:2], T.iot[:, 576:640], 0.0, None, MUL), 64, iB))
-    REV = T.mh[:, 1568:1696]
-    oR = dve(ts(REV, T.iot[:, 640:768], 0.0, None, EQ), 128, [iR], half=True)
-    IB = T.mb[:, 0:128]
-    oIB = dve(ts(IB, T.iot[:, 0:128], 0.0, None, EQ), 128, [iI], half=True)
-    oX = dve(ts(T.mb[:, 128:272], T.iot[:, 304:448], 0.0, None, EQ), 144, [iX], half=True)
-    w4 = [dve(ts(T.tmp[:, 32 * i:32 * i + 32], T.iot[:, 272:304], float(-i), WTS[i], EQ, MUL), 32, [iW]) for i in range(4)]
-    w2 = dve(tten(T.tmp[:, 128:192], T.tmp[:, 0:64], T.tmp[:, 64:128], ADD), 64, w4)
-    w1 = dve(tten(T.mb[:, 272:304], T.tmp[:, 128:160], T.tmp[:, 160:192], ADD), 64, [w2])
-    oW = [w1] + [dve(ts(T.mb[:, 304 + 32 * i:336 + 32 * i], T.mb[:, 272:304], s, None, MUL), 32, [w1]) for i, s in enumerate((16.0, -1.0, -16.0))]
-    WM = [T.mb[:, 272 + 32 * i:304 + 32 * i] for i in range(4)]
-    oZ = dve(mset(T.zb[:], 0.0), 544, [], half=True)
-    e4 = [dve(ts(T.tmp[:, 192 + 8 * i:200 + 8 * i], T.iot[:, 272:280], float(-i), None, EQ), 8, [iW]) for i in range(4)]
-    oS = [dve(tten(T.zb[:, 128 + 144 * t + 15:128 + 144 * t + 143:16], T.tmp[:, 192 + 8 * t:200 + 8 * t], T.tmp[:, 208 + 8 * t:216 + 8 * t], ADD), 8, e4 + [oZ]) for t in range(2)]
-    ZERO = T.zb[:, 0:128]
-    vm = dve(ts(T.Vm[:], T.V[:], 0.0625, -1.0, MUL, ADD), 2048, [lv], half=True)
-    lh = dve(cp(T.lph[:], T.lpi[:]), 256, [lp])
+    for i in range(4):
+        a, h, st = 1520 + 136 * i, i % 2, (-1, 1)[i // 2]
+        cur[0] = 2 + 3 * i
+        z = copy("late", M[:, a:a + 136], Z[:, 0:136], 136, [oZ])
+        cur[0] += 1
+        oB.append(mark("late", M[:, a + 1:a + 48:2], Z[:, 0:24], [[16, 3], [84, 2], [st, 4]], 3 * (st < 0) + 8 * h, 1.0, [z]))
+        cur[0] += 1
+        oB.append(mark("late", M[:, a + 49:a + 128:2], Z[:, 0:40], [[16, 5], [-44, 2], [st, 4]], 48 + 3 * (st < 0) + 8 * h, 1.0, [z]))
+    BM = [[M[:, 1520 + 136 * h + t:1648 + 136 * h + t] for h in range(2)] for t in range(2)]
+    BN = [[M[:, 1793 + 136 * h - t:1921 + 136 * h - t] for h in range(2)] for t in range(2)]
+    cur[0] = None
+    if OPT["vm"] == "act":
+        vm = act("vm", T.Vm[:], T.V[:], AF.Identity, [lv], bias=-1.0, scale=0.0625)
+    else:
+        vm = ts("vm", T.Vm[:], T.V[:], 0.0625, -1.0, MUL, ADD, [lv])
+    lh = cp("lh", T.lph[:], T.lpi[:], [lp])
+    l8 = ts("l8", T.lpq[:], T.lph[:], -1.0, 3.5 - 12288, MUL, ADD, [lh])
 
     ps = [T["ps%d" % b] for b in range(8)]
-    have = []
-    for q in range(NQ):
-        B = 2 * q + 1
-        mm = [pe([(ps[B][:, 320 + 32 * t:352 + 32 * t], AM[t][h], T.lph[:, 64 * q + h:64 * q + 64:2], h == 0, h == 1, 64) for h in range(2)], [lh, oA[t]], B) for t in range(2)]
-        have.append(dve(cp(T.lnd[:, 64 * q:64 * q + 64], ps[B][:, 320:384]), 64, mm, B))
 
+    def bank(kind, n):
+        if NQ <= 4:
+            return 2 * (n % NQ) + (kind == "pick")
+        return {"pick": n % 4, "sum": 4 + n % 2, "off": 6 + n % 2}[kind]
+
+    def group(out, terms):
+        return [(out, l, x, k == 0, k == len(terms) - 1) for k, (l, x) in enumerate(terms)]
+
+    have = [None] * NQ
     for r in range(RO):
         for q in range(NQ):
-            s = r * NQ + q
-            cur[0], cur[1] = s, len(ops)
-            A, B = 2 * q, 2 * q + 1
-            w = slice(WD * s, WD * s + WD)
-            LE, LF = T.lnd[:, 64 * s:64 * s + 32], T.lnd[:, 64 * s + 32:64 * s + 64]
-            HE, HF = T.l16[:, 64 * s:64 * s + 32], T.l16[:, 64 * s + 32:64 * s + 64]
-            got = have[q]
-            d1 = dve(cp(T.l16[:, 64 * s:64 * s + 64], T.lnd[:, 64 * s:64 * s + 64]), 64, [got])
-            Q = T.q16[:, 32 * s:32 * s + 32]
-            d2 = dve(ts(Q, LF, 0.125, 1024.5625, MUL, ADD), 32, [got])
-            o = ps[A][:, 0:32]
-            m1 = pe([(o, K16, HF, True, False, 64), (o, N16, Q, False, False, 64), (o, N16, CN, False, False, 64), (o, I16, HE, False, True, 64)], [d1, d2] + oI, A)
-            OF = T.off[:, 32 * s:32 * s + 32]
-            d3 = dve(cp(OF, o), 32, [m1], A)
-            gq = act(actf(T.wq[:, w], T.TB[:].indirect(OF), AF.Copy), GAM * WD + 35, [d3] + sb)
-            g1 = act(actf(T.g1[:, w], T.V[:].indirect(LE), AF.Copy), GAM * WD + 35, [got, lv])
-            s1 = dve(ts(T.s1[:, w], T.g1[:, w], -1.0, 1.0, ALU.max, ALU.min), WD, [g1], half=True)
-            p1 = dve(tten(T.p1[:, w], T.Vm[:].indirect(LF), T.s1[:, w], MUL), GAM * WD + 40, [s1, vm])
-            m2, d4 = [], []
-            for t in range(2):
-                m2.append(pe([(ps[B][:, 32 * t:32 * t + 32], T.zb[:, 128 + 144 * t + 15 - k:256 + 144 * t + 15 - k], T.wq[:, WD * s + k:WD * s + WD:16], k == 0, k == 15, 64) for k in range(16)],
-                             [gq, oS[t]], B))
-                d4.append(dve(cp(T.pro[:, 64 * s + 32 * t:64 * s + 32 * t + 32], ps[B][:, 32 * t:32 * t + 32]), 32, [m2[t]], B))
-            d5 = dve(tten(T.dl[:, 64 * s:64 * s + 64], ps[B][:, 0:64], T.l16[:, 64 * s:64 * s + 64], SUB), 64, m2 + [d1], B)
-            g2 = act(actf(T.g2[:, w], T.V[:].indirect(T.pro[:, 64 * s:64 * s + 32]), AF.Copy), GAM * WD + 35, [d4[0]])
-            s2 = dve(ts(T.s2[:, w], T.g2[:, w], -1.0, 1.0, ALU.max, ALU.min), WD, [g2], half=True)
-            p2 = dve(tten(T.p2[:, w], T.Vm[:].indirect(T.pro[:, 64 * s + 32:64 * s + 64]), T.s2[:, w], MUL), GAM * WD + 40, [s2, d4[1]])
-            pe([(ps[A][:, 128:256], IB, ZERO, True, False, 128)], [oIB, oZ], A)
-            for i, (buf, dep) in enumerate(((T.g1, g1), (T.p1, p1), (T.g2, g2), (T.p2, p2))):
-                m3 = pe([(ps[A][:, 128 + b:256:4], buf[:, WD * s + b:WD * s + WD:4], WM[i], False, i == 3 and b == 3, 64) for b in range(4)], [dep, oW[i]], A)
-            a1 = act(actf(T.ab[:, 128 * s:128 * s + 128], ps[A][:, 128:256], AF.Abs), 128, [m3], A)
-            m4 = pe([(ps[B][0:32, 128:256], T.ab[:, 128 * s + 32 * k:128 * s + 32 * k + 32], IB, k == 0, k == 3, 128) for k in range(4)], [a1], B)
-            a2 = act(actf(T.okb[0:32, 128 * s:128 * s + 128], ps[B][0:32, 128:256], AF.Relu, bias=1.0, scale=-1.0), 128, [m4], B)
-            m5 = [pe([(ps[B][:, 256 + 32 * t:288 + 32 * t], T.mb[0:32, 140 - 4 * a:268 - 4 * a], T.okb[0:32, 128 * s + a:128 * s + 128:4], a == 0, a == 3, 64) for a in range(4)],
-                     [a2, oX], B) for t in range(2)]
-            d6 = dve(tten(T.tt[:, 64 * s:64 * s + 64], ps[B][:, 256:320], T.dl[:, 64 * s:64 * s + 64], MUL), 64, m5 + [d5], B)
-            TE, TF = T.tt[:, 64 * s:64 * s + 32], T.tt[:, 64 * s + 32:64 * s + 64]
-            if r < RO - 1:
-                ME, MF, dm = (PG, PGP, oPG + oPP) if r % 2 == 0 else (PGM, PG, oPG + oPM)
-                oE, oF = ps[B][:, 320:352], ps[B][:, 352:384]
-                m6 = [pe([(oE, ME, HF, True, False, 64), (oE, ME, TF, False, True, 64)], [d6] + dm, B),
-                      pe([(oF, MF, HE, True, False, 64), (oF, MF, TE, False, True, 64)], [d6] + dm, B)]
+            s, C = r * NQ + q, CS[q]
+            cur[0] = s
+            b = 128 * r + LO[q]
+            WD = 16 * C
+            O, A, B = bank("off", s), bank("sum", s), bank("pick", s)
+            w, two, one = slice(16 * b, 16 * b + WD), slice(2 * b, 2 * b + 2 * C), slice(b, b + C)
+            e_, f_ = slice(2 * b, 2 * b + C), slice(2 * b + C, 2 * b + 2 * C)
+            OF, LE, LF, L2, L3 = (T.lst[:, 5 * b + C * i:5 * b + C * i + C] for i in range(5))
+            oo, oe, of = (ps[O][:, C * i:C * i + C] for i in range(3))
+            CQ, C1, CK = (M[:, 432 + 64 * i:432 + 64 * i + C] for i in range(3))
+            if r == 0:
+                x, x8 = ([buf[:, 2 * b + h:2 * b + 2 * C:2] for h in range(2)] for buf in (T.lph, T.lpq))
+                m1 = pe("m1", group(oo, [(AM[0][h], y) for y2 in ((CQ, CQ), x8, x) for h, y in enumerate(y2)] + [(AM[1][h], x[h]) for h in range(2)])
+                        + group(oe, [(AM[1][h], x[h]) for h in range(2)]) + group(of, [(AM[2][h], x[h]) for h in range(2)]), [l8, oC[0]] + oA, O)
             else:
-                m6 = [pe([(ps[B][:, 320 + h:384:2], BM[0][h], HE, True, False, 64), (ps[B][:, 320 + h:384:2], BM[1][h], HF, False, False, 64),
-                          (ps[B][:, 320 + h:384:2], BM[0][h], TE, False, False, 64), (ps[B][:, 320 + h:384:2], BM[1][h], TF, False, True, 64)], [d6] + oB, B) for h in range(2)]
-            d7 = dve(cp(T.snd[:, 64 * s:64 * s + 64], ps[B][:, 320:384]), 64, m6, B)
-            done.append(d7)
-            have[q] = op("pool", send(T.lnd[:, 64 * (s + NQ):64 * (s + NQ) + 64], T.snd[:, 64 * s:64 * s + 64], "ar%d" % s), REM_ISSUE, [d7],
-                         lat=REM_LAT, sem="ar%d" % s, val=n_eng, far=True)
+                le, lf = slice(2 * b - 256, 2 * b - 256 + C), slice(2 * b - 256 + C, 2 * b - 256 + 2 * C)
+                NE, NF, GE, GF = T.lnd[:, le], T.lnd[:, lf], T.neg[:, le], T.neg[:, lf]
+                d2 = ts("d2", T.q8[:, one], NE, -1.0, 3.5 - 12288, MUL, ADD, [have[q]])
+                dn = ts("dn", T.neg[:, le.start:lf.stop], T.lnd[:, le.start:lf.stop], 0.0, 2048.0, ALU.is_lt, MUL, [have[q]])
+                ME, MF, KF, dm = (PG, PGP, KP, oPG + oPP) if r % 2 == 1 else (PGM, PG, KG, oPG + oPM)
+                m1 = pe("m1", group(oo, [(KF, CQ), (KF, T.q8[:, one]), (KF, NE), (ME, NF), (ME, GF)])
+                        + group(oe, [(ME, NF), (ME, GF)]) + group(of, [(MF, NE), (MF, GE)]), [d2, dn] + dm, O)
+            d3 = cp("d3", T.lst[:, 5 * b:5 * b + 3 * C], ps[O][:, 0:3 * C], [m1], O)
+            gq = act("gq", T.wq[:, w], T.TB[:].indirect(OF), AF.Copy, [d3] + sb)
+            g1 = act("g1", T.g1[:, w], T.V[:].indirect(LE), AF.Copy, [d3, lv])
+            cut = 16 * b + WD * OPT["sa"] // 4
+            s1 = []
+            if cut > 16 * b:
+                s1.append(act("sa", T.s1[:, 16 * b:cut], T.g1[:, 16 * b:cut], AF.Sign, [g1]))
+            if cut < 16 * b + WD:
+                s1.append(ts("s1", T.s1[:, cut:16 * b + WD], T.g1[:, cut:16 * b + WD], -1.0, 1.0, ALU.max, ALU.min, [g1]))
+            p1 = tten("p1", T.p1[:, w], T.Vm[:].indirect(LF), T.s1[:, w], MUL, s1 + [vm])
+            Y, ye, yf, X = ps[B][:, 0:2 * C], ps[B][:, 0:C], ps[B][:, C:2 * C], ps[B][:, 128:128 + C]
+            F2, E2 = T.l16[:, 4 * b + 2 * C:4 * b + 3 * C], T.e16[:, one]
+            if OPT["pack"] == 1:
+                m2 = pe("m2", group(X, [(NK, C1)] + [(Z[:, 303 - k:431 - k], T.wq[:, 16 * b + k:16 * b + WD:16]) for k in range(16)]), [gq, oS, oI[0], oC[1]], B)
+                d40 = ts("d40", L2, X, 2048 + 1 / 4096 - 0.5, None, ADD, None, [m2], B)
+                d5 = ts("d5", T.l16[:, 4 * b:4 * b + 3 * C], T.lst[:, 5 * b + C:5 * b + 4 * C], -2048.0, None, ADD, None, [d40])
+                dx = tten("dx", E2, F2, X, SUB, [d5], B)
+                d41 = ts("d41", L3, E2, -2048.0, None, MUL, None, [dx])
+                pe("mo", [(Y, ZERO, Z[:, 0:2 * C], True, False), (ye, PI, CK, False, False), (ye, PI, F2, False, False), (yf, NK, E2, False, False)], [dx, oC[2]] + oI, B)
+            else:
+                X2 = ps[B][:, 128 + C:128 + 2 * C]
+                pick = [group(x, [(Z[:, a - k:a + 128 - k], T.wq[:, 16 * b + k:16 * b + WD:16]) for k in range(16)]) for x, a in ((X, 303), (X2, 1055))]
+                if OPT["pack"] == 0:
+                    if OPT["d40"] == "act":
+                        d40 = act("d40", L2, X, AF.Copy, [pe("m2", pick[0], [gq, oS], B)], B)
+                    else:
+                        d40 = cp("d40", L2, X, [pe("m2", pick[0], [gq, oS], B)], B)
+                    d41 = cp("d41", L3, X2, [pe("mx", pick[1], [gq, oS], B)], B)
+                else:
+                    d40 = d41 = cp("d40", T.lst[:, 5 * b + 3 * C:5 * b + 5 * C], ps[B][:, 128:128 + 2 * C], [pe("m2", pick[0] + pick[1], [gq, oS], B)], B)
+                d5 = ts("d5", T.l16[:, 4 * b:4 * b + 4 * C], T.lst[:, 5 * b + C:5 * b + 5 * C], -2048.0, None, ADD, None, [d41])
+                pe("mo", [(Y, PI, M[:, 560:560 + 2 * C], True, False), (Y, PI, T.l16[:, 4 * b + 2 * C:4 * b + 4 * C], False, False)], [d5, oC[2]] + oI, B)
+            sm = ps[A][:, 128:128 + 4 * C]
+            g2, p2 = [], []
+            cuts = (0, C // 4 * 2, C) if OPT["split"] else (0, C)
+            for u, (c0, c1) in enumerate(zip(cuts, cuts[1:])):
+                x, tag = slice(16 * (b + c0), 16 * (b + c1)), ("", "b")[u]
+                g2.append(act("g2" + tag, T.g2[:, x], T.V[:].indirect(T.lst[:, 5 * b + 3 * C + c0:5 * b + 3 * C + c1]), AF.Copy, [d40]))
+                s2 = ts("s2" + tag, T.s2[:, x], T.g2[:, x], -1.0, 1.0, ALU.max, ALU.min, g2[-1:])
+                p2.append(tten("p2" + tag, T.p2[:, x], T.Vm[:].indirect(T.lst[:, 5 * b + 4 * C + c0:5 * b + 4 * C + c1]), T.s2[:, x], MUL, [s2, d41]))
+            for i, (buf, dep) in enumerate(((T.g1, [g1]), (T.p1, [p1]), (T.g2, g2))):
+                pe("m3%d" % i, [(sm, WM[i][a], buf[:, 16 * b + a:16 * b + WD:4], i == 0 and a == 0, False) for a in range(4)], dep + oW, A)
+            for u, (c0, c1) in enumerate(zip(cuts, cuts[1:])):
+                m3 = pe("m33" + ("", "b")[u], [(ps[A][:, 128 + 4 * c0:128 + 4 * c1], WM[3][a], T.p2[:, 16 * (b + c0) + a:16 * (b + c1):4], False, c1 == C and a == 3) for a in range(4)], [p2[u]], A)
+            AB = T.ab[:, 4 * b:4 * b + 4 * C]
+            if OPT["absq"] == "act":
+                a1 = act("a1", AB, sm, AF.Abs, [m3], A)
+            else:
+                a1 = ts("a1", AB, sm, 0.0, None, ALU.not_equal, None, [m3], A)
+            m5 = pe("m5", [((ye, yf)[t], XM[a], T.ab[:, 4 * b + a:4 * b + 4 * C:4], False, t == 1 and a == 3) for t in range(2) for a in range(4)], [a1, oX], B)
+            d6 = tten("d6", T.snd[:, two], Y, T.l16[:, 4 * b:4 * b + 2 * C], ALU.max, [m5, d5], B)
+            done[s] = d6
+            have[q] = op("pool", "send", send(T.lnd[:, two], T.snd[:, two], "ar%d" % s), [d6], sem="ar%d" % s, val=n_eng, far=True)
 
-    n_st = 2 * NQ
+    n_st = len(OPT["stc"]) + len(OPT["stb"])
+    ycs, outs, c0 = [], [], [0, 0]
+    old = [done[s] for s in range(2 * NQ)]
+    FG, FS, FZ = T.wq, T.g1, T.s1
     for q in range(NQ):
-        s = NS + q
-        cur[0], cur[1] = s, len(ops)
-        B = 2 * q + 1
-        got = have[q]
-        outs = []
-        FG, FS, FZ = T.wq, T.g1, T.s1
+        C = CS[q]
+        cur[0] = NS + q
+        b = 2 * (LW - 128 + LO[q])
+        O, B = bank("off", NS + q), bank("pick", NS + q)
+        l0 = 5 * LW + 2 * LO[q]
+        yb, yc = slice(4 * LO[q], 4 * LO[q] + 4 * C), slice(2 * LO[q], 2 * LO[q] + 2 * C)
+        dn = ts("yn", T.neg[:, b:b + 2 * C], T.lnd[:, b:b + 2 * C], 0.0, 2048.0, ALU.is_lt, MUL, [have[q]])
+        src = [buf[:, b + C * t:b + C * t + C] for buf in (T.lnd, T.neg) for t in range(2)]
+        m = [pe(name, [mm for h in range(2) for mm in group(ps[k][:, h:2 * C:2], [(mat[i % 2][h], src[i]) for i in range(4)])], [dn] + oB, k)
+             for name, mat, k in (("yr", BM, O), ("ym", BN, B))]
+        got = cp("yl", T.lst[:, l0:l0 + 2 * C], ps[O][:, 0:2 * C], [m[0]], O)
+        c = act("yo", T.ycs[:, yc], ps[B][:, 0:2 * C], AF.Copy, [m[1]], B)
+        ycs.append(c)
+        if q in OPT["stc"]:
+            dma("sync", "st", T.yc[:, c0[0]:yc.stop], T.ycs[:, c0[0]:yc.stop], ycs, "sto", 16 * n_st)
+            c0[0] = yc.stop
+        fs = []
         for u in range(2):
-            a = 1024 * q + 512 * u
-            fg = act(actf(FG[:, a:a + 512], T.Vm[:].indirect(T.lnd[:, 64 * s + 32 * u:64 * s + 32 * u + 32]), AF.Copy), GAM * 512 + 35, [got, done[a // WD]])
-            fs = dve(ts(FS[:, a:a + 512], FG[:, a:a + 512], MAGIC + 1.0, MAGIC, ADD, SUB), 512, [fg], half=True)
-            fx = dve(tten(FG[:, a:a + 512:8], FG[:, a:a + 512:8], FS[:, a:a + 512:8], SUB), 128, [fs])
-            f0 = dve(mset(FS[:, a:a + 512:8], 0.0), 64, [fx])
-            sc = dve(lambda a=a: g.vector.tensor_tensor_scan(FZ[:, a:a + 512], FS[:, a:a + 512], FG[:, a:a + 512], 0.0, MUL, ADD), 512, [f0], half=True)
-            outs.append(act(actf(T.ybs[:, a // 8:a // 8 + 64], FZ[:, a + 7:a + 512:8], AF.Identity, bias=16.0, scale=16.0), 64, [sc]))
-        dma("sync", T.yb[:, 128 * q:128 * q + 128], T.ybs[:, 128 * q:128 * q + 128], outs, "sto", 16 * n_st, DMA_LAT)
-        d1 = dve(cp(T.l16[:, 64 * s:64 * s + 64], T.lnd[:, 64 * s:64 * s + 64]), 64, [got])
-        m = pe([(ps[B][:, 384:448], REV, T.l16[:, 64 * s:64 * s + 64], True, True, 64)], [d1, oR], B)
-        c = act(actf(T.ycs[:, 64 * q:64 * q + 64], ps[B][:, 384:448], AF.Copy), 64, [m], B)
-        dma("sync", T.yc[:, 64 * q:64 * q + 64], T.ycs[:, 64 * q:64 * q + 64], [c], "sto", 16 * n_st, DMA_LAT)
+            a, n = 32 * LO[q] + 16 * C * u, 16 * C
+            win = T.Vm[:].indirect(T.lst[:, l0 + C * u:l0 + C * u + C])
+            if u == 1 and q in OPT["fgd"]:
+                fg = cp("fg1", FG[:, a:a + n], win, [got] + old)
+            else:
+                fg = act("fg%d" % u, FG[:, a:a + n], win, AF.Copy, [got] + old)
+            fs.append(ts("fs%d" % u, FS[:, a:a + n], FG[:, a:a + n], MAGIC + 1.0, MAGIC, ADD, SUB, [fg]))
+        parts = 2 if q in OPT["half"] else 1
+        for u in range(2 - parts, 2):
+            n = 32 * C // parts
+            a = 32 * LO[q] + 32 * C - n * (2 - u)
+            fx = tten("fx%d" % u, FG[:, a:a + n:8], FG[:, a:a + n:8], FS[:, a:a + n:8], SUB, fs[:u + 1])
+            f0 = mset("fz%d" % u, FS[:, a:a + n:8], 0.0, [fx])
+            sc = op("dve", "sc%d" % u, lambda a=a, n=n: g.vector.tensor_tensor_scan(FZ[:, a:a + n], FS[:, a:a + n], FG[:, a:a + n], 0.0, MUL, ADD), [f0])
+            if OPT["foq"] == "act":
+                outs.append(act("fo%d" % u, T.ybs[:, a // 8:(a + n) // 8], FZ[:, a + 7:a + n:8], AF.Identity, [sc], bias=16.0, scale=16.0))
+            else:
+                outs.append(ts("fo%d" % u, T.ybs[:, a // 8:(a + n) // 8], FZ[:, a + 7:a + n:8], 16.0, 16.0, MUL, ADD, [sc]))
+        if q in OPT["stb"]:
+            dma("sync", "sb", T.yb[:, c0[1]:yb.stop], T.ybs[:, c0[1]:yb.stop], outs, "sto", 16 * n_st)
+            c0[1] = yb.stop
     return ops
 
 
 def schedule(ops):
-    order = [62 * DIGITS.index(ORDER[k]) + DIGITS.index(ORDER[k + 1]) for k in range(0, len(ORDER), 2)]
-    place = {i: k for k, i in enumerate(order)}
-    assert len(place) == len(ops) and all(place[d] < place[i] for i, o in enumerate(ops) for d in o["deps"] + o["after"])
+    key = []
+    for o in ops:
+        n, name = o["beat"], o["name"]
+        if n is None:
+            t = ONCE[name]
+        elif n < NQ and name in EARLY:
+            t = EARLY[name] + EARLY["gap"] * n
+        elif n < NQ:
+            t = FIRST[name] + FIRST["step"] * n
+        else:
+            t = TIME[name] + n
+        key.append(t)
+    lines = {}
+    for i in sorted(range(len(ops)), key=lambda i: (-key[i], -i)):
+        lines.setdefault(ops[i]["eng"], []).append(i)
+    order, out = [], set()
+    while len(order) < len(ops):
+        n = len(order)
+        for line in lines.values():
+            while line and out.issuperset(ops[line[-1]]["deps"] + ops[line[-1]]["after"]):
+                out.add(line[-1])
+                order.append(line.pop())
+        if len(order) == n:
+            return None
     return order
 
 

from concourse.mybir import AluOpType as ALU, ActivationFunctionType as AF

RO = 5
CS = (32, 32, 32, 32)
NQ = len(CS)
LO = [sum(CS[:q]) for q in range(NQ)]
NS = NQ * RO
BF, H, F, I32, U = "bfloat16", "float16", "float32", "int32", "uint16"
WTS = (1.0, 61.0, 3728.0, 228352.0)
MAGIC = 12582912.0
LW = 128 * RO

SCRATCH = {
    "V": ("sbuf", [128, 2048], BF), "Vm": ("sbuf", [128, 2048], BF), "TB": ("sbuf", [128, 16384], BF),
    "sqi": ("sbuf", [128, 256], I32), "hl": ("sbuf", [128, 512], BF), "stage": ("dram", [4, 16384], BF),
    "lpi": ("sbuf", [128, 256], I32), "lph": ("sbuf", [128, 256], H), "lpq": ("sbuf", [128, 256], H),
    "zb": ("sbuf", [128, 1184], BF), "mt": ("sbuf", [128, 2080], H),
    "lnd": ("sbuf", [128, 2 * LW], H), "snd": ("sbuf", [128, 2 * LW], H), "neg": ("sbuf", [128, 2 * LW], H),
    "lst": ("sbuf", [128, 5 * LW + 256], U),
    "l16": ("sbuf", [128, 4 * LW], H), "q8": ("sbuf", [128, LW], H), "e16": ("sbuf", [128, LW], H),
    "ab": ("sbuf", [128, 4 * LW], BF),
    "ycs": ("sbuf", [128, 256], F), "ybs": ("sbuf", [128, 512], F),
}
for _n in ("wq", "g1", "s1", "p1", "g2", "s2", "p2"):
    SCRATCH[_n] = ("sbuf", [128, 16 * LW], BF)
for _b in range(8):
    SCRATCH["ps%d" % _b] = ("psum", [128, 512], F)
SEMAPHORES = ["pe", "dve", "act", "pool", "ldq", "ldp", "ldv", "fill", "sta", "stb", "sto", "loc"] + ["ar%d" % i for i in range(NS)]

OPT = dict(split=0, d40="dve", stc=(3,), stb=(1, 2, 3), fgd=(3,), half=(3,), sa=0, pack=0, foq="act", ta=2, f0=4, fd=9, fa=3, fp=2, vm="act", okq="act", absq="act")

TIME = dict(d2=-0.326, dn=-0.321, m1=-0.316, d3=0.114, gq=0.12, g1=0.125, s1=0.683, sa=0.7, p1=1.118, m2=0.681, d40=0.682, d5=1.688, dx=0.95, mx=0.689, d41=1.144, mo=1.962,
            g2=1.049, s2=1.148, p2=1.41, m30=1.68, m31=1.68, m32=1.684, m33=1.688, a1=2.061, m5=2.062, d6=2.229, send=2.3, late=2.4,
            yn=-0.32, yr=-0.307, ym=0.684, yl=0.127, yo=1.03, st=1.1, fg0=0.13, fg1=0.14, fs0=1.127, fs1=1.13, fx0=1.13, fx1=1.424, fz0=1.23, fz1=1.683, sc0=1.674, sc1=2.13, fo0=2.2, fo1=2.3, sb=2.4)
EARLY = dict(m1=-3.0, d3=-2.9, g1=-2.0, s1=-1.9, p1=-1.85, gap=0.1)
FIRST = dict(gq=-0.731, m2=-0.124, d40=0.311, mx=0.716, d41=0.72, d5=0.73, mo=1.24, g2=0.312, s2=0.736, p2=1.49, m30=1.206, m31=1.568, m32=1.751, m33=1.752,
             a1=1.981, m5=2.129, d6=2.43, send=2.44, late=3.212, step=0.958)
ONCE = dict(zero=-30.0, load=-34.0, filld=-25.0, fille=-6.0, filla=-12.0, hi=-10.0, vm=-9.0, lh=-8.0, l8=-2.95, stage=-5.0, table=-4.0, tabla=-4.0, ma0=-20.0, fillp=-19.0, mat=-18.0, wm=-1.0)
OPT.update(stc=(1, 3), stb=(0, 1, 2, 3), fgd=(), half=(0, 1, 2, 3))
TIME.update(yr=-0.4416, m1=-0.4376, d2=-0.416, dn=-0.1843, yn=-0.1767, fg0=0.0468, d3=0.0584, yl=0.0637, gq=0.0646, ym=0.3613, m2=0.3749, g1=0.3764, sa=0.7, d40=0.8385, fs0=0.8477, s1=0.851, mx=0.8863, g2=0.9177, fg1=0.9239, yo=0.9367, dx=0.95, m30=1.0038, m31=1.0207, p1=1.0698, fx0=1.1437, fs1=1.1581, fz0=1.1655, s2=1.2891, d41=1.3035, send=1.4138, fx1=1.5557, m32=1.6654, sc0=1.8069, fz1=1.8104, p2=1.8347, m33=1.869, d5=1.9677, mo=2.0111, m5=2.0148, a1=2.0282, sc1=2.0607, late=2.4, d6=2.4948, st=3.0174, fo0=4.9958, fo1=5.501, sb=8.4394)
FIRST.update(m2=-2.5643, gq=-2.3448, late=0.3, d40=-1.3664, mx=-0.8627, d41=-0.2159, g2=-0.1188, send=0.169, m30=0.2583, m31=0.4495, m32=0.6463, s2=0.663, m33=0.7454, p2=0.7533, d5=0.8701, mo=1.0644, step=1.1066, a1=1.1693, m5=1.3099, d6=1.7768)
EARLY.update(g1=-3.4012, m1=-2.6935, d3=-2.317, s1=-1.7403, p1=-1.1938, gap=-0.3188)
ONCE.update(load=-33.9596, stage=-33.9532, table=-33.951, filld=-24.5007, zero=-24.6, hi=-24.3489, fille=-21.6925, lh=-21.6898, l8=-21.6454, fillp=-18.3, ma0=-18.3914, mat=-18.2, filla=-10.8913, vm=-10.7232, tabla=-10.7145, wm=-0.5164)
TIME.update(m1=-0.4376, d2=-0.416, yr=-0.3137, yn=-0.221, dn=-0.1843, yl=0.0072, d3=0.0584, gq=0.0646, fg0=0.3473, ym=0.3625, fg1=0.3638, m2=0.3749, g1=0.3764, sa=0.7, d40=0.8385, s1=0.851, mx=0.8863, g2=0.9177, yo=0.9411, dx=0.95, fs0=0.9659, m30=1.0038, fx0=1.0195, m31=1.0207, fs1=1.0299, p1=1.0698, fz0=1.2422, s2=1.2891, d41=1.3035, send=1.4138, fx1=1.5092, m32=1.6654, sc0=1.7269, fz1=1.7424, p2=1.8347, m33=1.869, fo0=1.9466, fo1=1.9501, d5=1.9677, sc1=1.9716, mo=2.0111, m5=2.0148, a1=2.0282, late=2.4, d6=2.4948, st=5.5666, sb=6.5788)
FIRST.update(m30=-2.6426, m2=-1.2616, d40=-0.7226, gq=-0.6722, mx=-0.4486, send=-0.0151, d41=0.2488, s2=0.2624, late=0.3, g2=0.4073, m31=0.54, m32=0.701, m33=0.7173, step=1.0749, mo=1.1182, p2=1.2391, d5=1.2473, m5=1.4121, a1=1.4863, d6=1.8753)
EARLY.update(m1=-4.8904, d3=-3.9577, g1=-0.813, s1=-0.7792, p1=-0.7624, gap=0.0179)
ONCE.update(load=-38, stage=-37, table=-36, zero=-30, filld=-29, hi=-28, lh=-27, l8=-25, fille=-26, wm=-1, fillp=-17, ma0=-18, mat=-16, filla=-3, vm=-2, tabla=-1)
FIRST.update(gq=-2.0633, m2=-1.8185, mx=-0.7396, d40=-0.7041, d41=-0.1993, s2=-0.1932, g2=0.1252, m30=0.3332, send=0.3425, m31=0.3449, late=0.35, m32=0.3513, m33=0.3717, p2=0.8851, d5=0.9001, step=1.107, mo=1.1187, a1=1.2393, m5=1.3245, d6=1.7964)
EARLY.update(d3=-8.6204, g1=-3.2076, m1=-2.2665, s1=-0.8843, p1=-0.8287, gap=0.044)
ONCE.update(load=-37.3197, stage=-37.1808, table=-37.163, filld=-28.8134, hi=-28.5992, zero=-28.2568, fille=-28.2541, lh=-28.2222, l8=-28.2056, fillp=-18.1182, ma0=-18.1126, mat=-18.1094, filla=-4.1238, vm=-4.1155, tabla=-4.097, wm=-0.75)


def build(g, T, send, n_eng):
    ops = []
    banks = {}
    done = {}
    cur = [None]

    def op(eng, name, fn, deps=(), bank=None, after=(), sem=None, val=None, far=False):
        deps = [d for d in deps if d is not None]
        after = [d for d in after if d is not None]
        if bank is not None:
            last = banks.setdefault(bank, {})
            for e, d in last.items():
                (after if e == eng else deps).append(d)
            last[eng] = len(ops)
        ops.append(dict(beat=cur[0], name=name, eng=eng, fn=fn, deps=sorted(set(deps)), after=after, sem=sem, val=val, far=far))
        return len(ops) - 1

    def pe(name, mms, deps, bank):
        def fn():
            for m in mms:
                ins = g.tensor.matmul(*m)
            return ins
        return op("pe", name, fn, deps, bank)

    def dma(eng, name, out, in_, deps, sem, val):
        q = g.sync if eng == "sync" else g.scalar
        return op(eng, name, lambda: q.dma_start(out, in_), deps, sem=sem, val=val)

    def ts(name, out, in0, a, b, o0, o1, deps, bank=None):
        if o1 is None:
            return op("dve", name, lambda: g.vector.tensor_scalar(out, in0, a, None, o0), deps, bank)
        return op("dve", name, lambda: g.vector.tensor_scalar(out, in0, a, b, o0, o1), deps, bank)

    def tten(name, out, in0, in1, o, deps, bank=None):
        return op("dve", name, lambda: g.vector.tensor_tensor(out, in0, in1, o), deps, bank)

    def cp(name, out, in_, deps, bank=None):
        return op("dve", name, lambda: g.vector.tensor_copy(out, in_), deps, bank)

    def mset(name, ap, c, deps=()):
        return op("dve", name, lambda: g.vector.memset(ap, c), deps)

    def act(name, out, in_, f, deps, bank=None, **kw):
        return op("act", name, lambda: g.scalar.activation(out, in_, f, **kw), deps, bank)

    EQ, MUL, ADD, SUB = ALU.is_equal, ALU.mult, ALU.add, ALU.subtract

    def sel(name, out, in_, pat, cmp, fill, base, cm, deps):
        return op("pool", name, lambda: g.affine_select(out, in_, pat, cmp, fill, base, cm), deps)

    def mark(name, out, in_, pat, base, c, deps):
        return sel(name, out, in_, pat, ALU.not_equal, c, base, -1, deps)

    def copy(name, out, in_, n, deps):
        return sel(name, out, in_, [[0, n]], ALU.is_ge, 0.0, 0, 0, deps)

    lq = dma("sync", "load", T.sqi[:], T.sq[:], [], "ldq", 16)
    lp = dma("sync", "load", T.lpi[:], T.lp[:], [], "ldp", 16)
    oZ = mset("zero", T.zb[:], 0.0)
    lv = dma("act", "load", T.V[:], T.v[:], [], "ldv", 16)
    nd, na = OPT["fd"], OPT["fa"]
    fills = [mset("filld" if k < OPT["f0"] else "fille", T.TB[:, 1024 * k:1024 * k + 1024], 0.0) for k in range(nd)]
    afill = [act("filla", T.TB[:, 1024 * k:1024 * k + 1024], T.TB[:, 0:1024], AF.Copy, fills[:1]) for k in range(nd, nd + na)]
    fills += afill
    nf = nd + na + OPT["fp"]
    if OPT["fp"]:
        fills.append(op("pool", "fillp", lambda: g.iota(T.TB[:, 1024 * (nd + na):1024 * nf], [[0, 1024 * OPT["fp"]]], 0, 0, allow_small_or_imprecise_dtypes=True)))
    for k in range(nf // 2, 8):
        fills.append(dma("sync", "load", T.TB[:, 2048 * k:2048 * k + 2048], T.v[:], [], "fill", 16 * (8 - nf // 2)))
    hi = cp("hi", T.hl[:, 0:256], T.sqi[:], [lq])
    lo = tten("hi", T.hl[:, 256:512], T.sqi[:], T.hl[:, 0:256], SUB, [hi])
    sa = [dma("sync", "stage", T.stage[0:2, :], T.hl[:, 0:256], [hi], "sta", 32),
          dma("sync", "stage", T.stage[2:4, :], T.hl[:, 256:512], [lo], "sta", 32)]
    sb = [dma("act" if k < OPT["ta"] else "sync", "tabla" if k < OPT["ta"] else "table", T.TB[16 * k:16 * k + 4, :], T.stage[:], sa + fills, "stb", 128) for k in range(8)]

    Z = T.zb
    ZERO = Z[:, 0:128]
    M = T.mt
    AM, oA = [], []
    for i, (t, c) in enumerate(((1, 2048.0), (0, 1.0), (1, 1.0))):
        oA.append(mark("ma0", M[:, 144 * i:144 * i + 144], Z[:, 0:144], [[16, 9], [-1000, 2], [2, 8]], 1000 + t, c, [oZ]))
        AM.append([M[:, 144 * i + 8 * (1 - h):144 * i + 128 + 8 * (1 - h)] for h in range(2)])
    oC = [sel("mat" if i else "ma0", M[:, 432 + 64 * i:496 + 64 * i], Z[:, 0:64], [[0, 64]], ALU.is_gt, c, 0, 0, [oZ]) for i, c in enumerate((12288.0, 1.0, 2048.0))]
    NK, PI = M[:, 624:752], M[:, 752:880]
    w0 = 432 + 96
    XP = [[-4, 9], [1000, 4], [-32, 4]]
    oS = oW = oX = oZ
    oI = []
    for i in range(4):
        oW = mark("mat", Z[:, w0:w0 + 32], Z[:, w0:w0 + 32], [[16, 8], [4, 4]], i, WTS[i], [oW])
        col = Z[:, 303:431:16] if OPT["pack"] == 1 or i % 2 == 0 else Z[:, 1055:1183:16]
        oS = mark("mat", col, col, [[16, 8]], i, (1.0, 1 / 2048)[i % 2] if OPT["pack"] == 1 else 1.0, [oS])
        if i % 2 == 0:
            oI.append(mark("mat", (NK, PI)[i // 2], ZERO, [[1, 128]], 0, (-2048.0, 1.0)[i // 2], [oZ]))
        else:
            oX = sel("mat", Z[:, 144:288], Z[:, 144:288], XP, ALU.is_ge, (-4096.0, 0.0)[i // 2], 4 * (i // 2), 1, [oX])
    oW = [oW] + [ts("wm", Z[:, w0 + 128 * i:w0 + 128 * i + 32], Z[:, w0:w0 + 32], c, None, MUL, None, [oW]) for i, c in ((1, 16.0), (2, -1.0), (3, -16.0))]
    WM = [[Z[:, w0 + 128 * i - 32 * a:w0 + 128 * i - 32 * a + 128] for a in range(4)] for i in range(4)]
    XM = [Z[:, 160 - 4 * b:288 - 4 * b] for b in range(4)]
    PG, KG, PGP, KP, PGM = (M[:, a:a + 128] for a in (880, 1008, 1136, 1264, 1392))
    oPG = [mark("mat", M[:, m + a:m + a + n], Z[:, 0:n], [[8, n // 8], [st, 2], [1, 4]], a, c, [oZ])
           for m, c in ((880, 1.0), (1008, 2048.0)) for a, n, st in ((0, 48, 84), (48, 80, -44))]
    z = [copy("mat", M[:, m + 256:m + 383], M[:, m + 1:m + 128], 127, oPG) for m in (880, 1008)]
    oPP = [copy("mat", M[:, m + 259:m + 384:4], M[:, m:m + 128:4], 32, z) for m in (880, 1008)]
    cur[0] = 0
    z = copy("late", M[:, 1393:1520], M[:, 880:1007], 127, oPG)
    cur[0] = 1
    oPM = [copy("late", M[:, 1392:1520:4], M[:, 883:1008:4], 32, [z])]
    oB = []
    for i in range(4):
        a, h, st = 1520 + 136 * i, i % 2, (-1, 1)[i // 2]
        cur[0] = 2 + 3 * i
        z = copy("late", M[:, a:a + 136], Z[:, 0:136], 136, [oZ])
        cur[0] += 1
        oB.append(mark("late", M[:, a + 1:a + 48:2], Z[:, 0:24], [[16, 3], [84, 2], [st, 4]], 3 * (st < 0) + 8 * h, 1.0, [z]))
        cur[0] += 1
        oB.append(mark("late", M[:, a + 49:a + 128:2], Z[:, 0:40], [[16, 5], [-44, 2], [st, 4]], 48 + 3 * (st < 0) + 8 * h, 1.0, [z]))
    BM = [[M[:, 1520 + 136 * h + t:1648 + 136 * h + t] for h in range(2)] for t in range(2)]
    BN = [[M[:, 1793 + 136 * h - t:1921 + 136 * h - t] for h in range(2)] for t in range(2)]
    cur[0] = None
    if OPT["vm"] == "act":
        vm = act("vm", T.Vm[:], T.V[:], AF.Identity, [lv], bias=-1.0, scale=0.0625)
    else:
        vm = ts("vm", T.Vm[:], T.V[:], 0.0625, -1.0, MUL, ADD, [lv])
    lh = cp("lh", T.lph[:], T.lpi[:], [lp])
    l8 = ts("l8", T.lpq[:], T.lph[:], -1.0, 3.5 - 12288, MUL, ADD, [lh])

    ps = [T["ps%d" % b] for b in range(8)]

    def bank(kind, n):
        if NQ <= 4:
            return 2 * (n % NQ) + (kind == "pick")
        return {"pick": n % 4, "sum": 4 + n % 2, "off": 6 + n % 2}[kind]

    def group(out, terms):
        return [(out, l, x, k == 0, k == len(terms) - 1) for k, (l, x) in enumerate(terms)]

    have = [None] * NQ
    for r in range(RO):
        for q in range(NQ):
            s, C = r * NQ + q, CS[q]
            cur[0] = s
            b = 128 * r + LO[q]
            WD = 16 * C
            O, A, B = bank("off", s), bank("sum", s), bank("pick", s)
            w, two, one = slice(16 * b, 16 * b + WD), slice(2 * b, 2 * b + 2 * C), slice(b, b + C)
            e_, f_ = slice(2 * b, 2 * b + C), slice(2 * b + C, 2 * b + 2 * C)
            OF, LE, LF, L2, L3 = (T.lst[:, 5 * b + C * i:5 * b + C * i + C] for i in range(5))
            oo, oe, of = (ps[O][:, C * i:C * i + C] for i in range(3))
            CQ, C1, CK = (M[:, 432 + 64 * i:432 + 64 * i + C] for i in range(3))
            if r == 0:
                x, x8 = ([buf[:, 2 * b + h:2 * b + 2 * C:2] for h in range(2)] for buf in (T.lph, T.lpq))
                m1 = pe("m1", group(oo, [(AM[0][h], y) for y2 in ((CQ, CQ), x8, x) for h, y in enumerate(y2)] + [(AM[1][h], x[h]) for h in range(2)])
                        + group(oe, [(AM[1][h], x[h]) for h in range(2)]) + group(of, [(AM[2][h], x[h]) for h in range(2)]), [l8, oC[0]] + oA, O)
            else:
                le, lf = slice(2 * b - 256, 2 * b - 256 + C), slice(2 * b - 256 + C, 2 * b - 256 + 2 * C)
                NE, NF, GE, GF = T.lnd[:, le], T.lnd[:, lf], T.neg[:, le], T.neg[:, lf]
                d2 = ts("d2", T.q8[:, one], NE, -1.0, 3.5 - 12288, MUL, ADD, [have[q]])
                dn = ts("dn", T.neg[:, le.start:lf.stop], T.lnd[:, le.start:lf.stop], 0.0, 2048.0, ALU.is_lt, MUL, [have[q]])
                ME, MF, KF, dm = (PG, PGP, KP, oPG + oPP) if r % 2 == 1 else (PGM, PG, KG, oPG + oPM)
                m1 = pe("m1", group(oo, [(KF, CQ), (KF, T.q8[:, one]), (KF, NE), (ME, NF), (ME, GF)])
                        + group(oe, [(ME, NF), (ME, GF)]) + group(of, [(MF, NE), (MF, GE)]), [d2, dn] + dm, O)
            d3 = cp("d3", T.lst[:, 5 * b:5 * b + 3 * C], ps[O][:, 0:3 * C], [m1], O)
            gq = act("gq", T.wq[:, w], T.TB[:].indirect(OF), AF.Copy, [d3] + sb)
            g1 = act("g1", T.g1[:, w], T.V[:].indirect(LE), AF.Copy, [d3, lv])
            cut = 16 * b + WD * OPT["sa"] // 4
            s1 = []
            if cut > 16 * b:
                s1.append(act("sa", T.s1[:, 16 * b:cut], T.g1[:, 16 * b:cut], AF.Sign, [g1]))
            if cut < 16 * b + WD:
                s1.append(ts("s1", T.s1[:, cut:16 * b + WD], T.g1[:, cut:16 * b + WD], -1.0, 1.0, ALU.max, ALU.min, [g1]))
            p1 = tten("p1", T.p1[:, w], T.Vm[:].indirect(LF), T.s1[:, w], MUL, s1 + [vm])
            Y, ye, yf, X = ps[B][:, 0:2 * C], ps[B][:, 0:C], ps[B][:, C:2 * C], ps[B][:, 128:128 + C]
            F2, E2 = T.l16[:, 4 * b + 2 * C:4 * b + 3 * C], T.e16[:, one]
            if OPT["pack"] == 1:
                m2 = pe("m2", group(X, [(NK, C1)] + [(Z[:, 303 - k:431 - k], T.wq[:, 16 * b + k:16 * b + WD:16]) for k in range(16)]), [gq, oS, oI[0], oC[1]], B)
                d40 = ts("d40", L2, X, 2048 + 1 / 4096 - 0.5, None, ADD, None, [m2], B)
                d5 = ts("d5", T.l16[:, 4 * b:4 * b + 3 * C], T.lst[:, 5 * b + C:5 * b + 4 * C], -2048.0, None, ADD, None, [d40])
                dx = tten("dx", E2, F2, X, SUB, [d5], B)
                d41 = ts("d41", L3, E2, -2048.0, None, MUL, None, [dx])
                pe("mo", [(Y, ZERO, Z[:, 0:2 * C], True, False), (ye, PI, CK, False, False), (ye, PI, F2, False, False), (yf, NK, E2, False, False)], [dx, oC[2]] + oI, B)
            else:
                X2 = ps[B][:, 128 + C:128 + 2 * C]
                pick = [group(x, [(Z[:, a - k:a + 128 - k], T.wq[:, 16 * b + k:16 * b + WD:16]) for k in range(16)]) for x, a in ((X, 303), (X2, 1055))]
                if OPT["pack"] == 0:
                    if OPT["d40"] == "act":
                        d40 = act("d40", L2, X, AF.Copy, [pe("m2", pick[0], [gq, oS], B)], B)
                    else:
                        d40 = cp("d40", L2, X, [pe("m2", pick[0], [gq, oS], B)], B)
                    d41 = cp("d41", L3, X2, [pe("mx", pick[1], [gq, oS], B)], B)
                else:
                    d40 = d41 = cp("d40", T.lst[:, 5 * b + 3 * C:5 * b + 5 * C], ps[B][:, 128:128 + 2 * C], [pe("m2", pick[0] + pick[1], [gq, oS], B)], B)
                d5 = ts("d5", T.l16[:, 4 * b:4 * b + 4 * C], T.lst[:, 5 * b + C:5 * b + 5 * C], -2048.0, None, ADD, None, [d41])
                pe("mo", [(Y, PI, M[:, 560:560 + 2 * C], True, False), (Y, PI, T.l16[:, 4 * b + 2 * C:4 * b + 4 * C], False, False)], [d5, oC[2]] + oI, B)
            sm = ps[A][:, 128:128 + 4 * C]
            g2, p2 = [], []
            cuts = (0, C // 4 * 2, C) if OPT["split"] else (0, C)
            for u, (c0, c1) in enumerate(zip(cuts, cuts[1:])):
                x, tag = slice(16 * (b + c0), 16 * (b + c1)), ("", "b")[u]
                g2.append(act("g2" + tag, T.g2[:, x], T.V[:].indirect(T.lst[:, 5 * b + 3 * C + c0:5 * b + 3 * C + c1]), AF.Copy, [d40]))
                s2 = ts("s2" + tag, T.s2[:, x], T.g2[:, x], -1.0, 1.0, ALU.max, ALU.min, g2[-1:])
                p2.append(tten("p2" + tag, T.p2[:, x], T.Vm[:].indirect(T.lst[:, 5 * b + 4 * C + c0:5 * b + 4 * C + c1]), T.s2[:, x], MUL, [s2, d41]))
            for i, (buf, dep) in enumerate(((T.g1, [g1]), (T.p1, [p1]), (T.g2, g2))):
                pe("m3%d" % i, [(sm, WM[i][a], buf[:, 16 * b + a:16 * b + WD:4], i == 0 and a == 0, False) for a in range(4)], dep + oW, A)
            for u, (c0, c1) in enumerate(zip(cuts, cuts[1:])):
                m3 = pe("m33" + ("", "b")[u], [(ps[A][:, 128 + 4 * c0:128 + 4 * c1], WM[3][a], T.p2[:, 16 * (b + c0) + a:16 * (b + c1):4], False, c1 == C and a == 3) for a in range(4)], [p2[u]], A)
            AB = T.ab[:, 4 * b:4 * b + 4 * C]
            if OPT["absq"] == "act":
                a1 = act("a1", AB, sm, AF.Abs, [m3], A)
            else:
                a1 = ts("a1", AB, sm, 0.0, None, ALU.not_equal, None, [m3], A)
            m5 = pe("m5", [((ye, yf)[t], XM[a], T.ab[:, 4 * b + a:4 * b + 4 * C:4], False, t == 1 and a == 3) for t in range(2) for a in range(4)], [a1, oX], B)
            d6 = tten("d6", T.snd[:, two], Y, T.l16[:, 4 * b:4 * b + 2 * C], ALU.max, [m5, d5], B)
            done[s] = d6
            have[q] = op("pool", "send", send(T.lnd[:, two], T.snd[:, two], "ar%d" % s), [d6], sem="ar%d" % s, val=n_eng, far=True)

    n_st = len(OPT["stc"]) + len(OPT["stb"])
    ycs, outs, c0 = [], [], [0, 0]
    old = [done[s] for s in range(2 * NQ)]
    FG, FS, FZ = T.wq, T.g1, T.s1
    for q in range(NQ):
        C = CS[q]
        cur[0] = NS + q
        b = 2 * (LW - 128 + LO[q])
        O, B = bank("off", NS + q), bank("pick", NS + q)
        l0 = 5 * LW + 2 * LO[q]
        yb, yc = slice(4 * LO[q], 4 * LO[q] + 4 * C), slice(2 * LO[q], 2 * LO[q] + 2 * C)
        dn = ts("yn", T.neg[:, b:b + 2 * C], T.lnd[:, b:b + 2 * C], 0.0, 2048.0, ALU.is_lt, MUL, [have[q]])
        src = [buf[:, b + C * t:b + C * t + C] for buf in (T.lnd, T.neg) for t in range(2)]
        m = [pe(name, [mm for h in range(2) for mm in group(ps[k][:, h:2 * C:2], [(mat[i % 2][h], src[i]) for i in range(4)])], [dn] + oB, k)
             for name, mat, k in (("yr", BM, O), ("ym", BN, B))]
        got = cp("yl", T.lst[:, l0:l0 + 2 * C], ps[O][:, 0:2 * C], [m[0]], O)
        c = act("yo", T.ycs[:, yc], ps[B][:, 0:2 * C], AF.Copy, [m[1]], B)
        ycs.append(c)
        if q in OPT["stc"]:
            dma("sync", "st", T.yc[:, c0[0]:yc.stop], T.ycs[:, c0[0]:yc.stop], ycs, "sto", 16 * n_st)
            c0[0] = yc.stop
        fs = []
        for u in range(2):
            a, n = 32 * LO[q] + 16 * C * u, 16 * C
            win = T.Vm[:].indirect(T.lst[:, l0 + C * u:l0 + C * u + C])
            if u == 1 and q in OPT["fgd"]:
                fg = cp("fg1", FG[:, a:a + n], win, [got] + old)
            else:
                fg = act("fg%d" % u, FG[:, a:a + n], win, AF.Copy, [got] + old)
            fs.append(ts("fs%d" % u, FS[:, a:a + n], FG[:, a:a + n], MAGIC + 1.0, MAGIC, ADD, SUB, [fg]))
        parts = 2 if q in OPT["half"] else 1
        for u in range(2 - parts, 2):
            n = 32 * C // parts
            a = 32 * LO[q] + 32 * C - n * (2 - u)
            fx = tten("fx%d" % u, FG[:, a:a + n:8], FG[:, a:a + n:8], FS[:, a:a + n:8], SUB, fs[:u + 1])
            f0 = mset("fz%d" % u, FS[:, a:a + n:8], 0.0, [fx])
            sc = op("dve", "sc%d" % u, lambda a=a, n=n: g.vector.tensor_tensor_scan(FZ[:, a:a + n], FS[:, a:a + n], FG[:, a:a + n], 0.0, MUL, ADD), [f0])
            if OPT["foq"] == "act":
                outs.append(act("fo%d" % u, T.ybs[:, a // 8:(a + n) // 8], FZ[:, a + 7:a + n:8], AF.Identity, [sc], bias=16.0, scale=16.0))
            else:
                outs.append(ts("fo%d" % u, T.ybs[:, a // 8:(a + n) // 8], FZ[:, a + 7:a + n:8], 16.0, 16.0, MUL, ADD, [sc]))
        if q in OPT["stb"]:
            dma("sync", "sb", T.yb[:, c0[1]:yb.stop], T.ybs[:, c0[1]:yb.stop], outs, "sto", 16 * n_st)
            c0[1] = yb.stop
    return ops


def schedule(ops):
    key = []
    for o in ops:
        n, name = o["beat"], o["name"]
        if n is None:
            t = ONCE[name]
        elif n < NQ and name in EARLY:
            t = EARLY[name] + EARLY["gap"] * n
        elif n < NQ:
            t = FIRST[name] + FIRST["step"] * n
        else:
            t = TIME[name] + n
        key.append(t)
    lines = {}
    for i in sorted(range(len(ops)), key=lambda i: (-key[i], -i)):
        lines.setdefault(ops[i]["eng"], []).append(i)
    order, out = [], set()
    while len(order) < len(ops):
        n = len(order)
        for line in lines.values():
            while line and out.issuperset(ops[line[-1]]["deps"] + ops[line[-1]]["after"]):
                out.add(line[-1])
                order.append(line.pop())
        if len(order) == n:
            return None
    return order


def emit(g, T, ops, order):
    queue = {"pe": g.tensor, "dve": g.vector, "act": g.scalar, "pool": g, "sync": g.sync}
    count = {"pe": 0, "dve": 0, "act": 0, "pool": 0}
    seen = {e: {} for e in queue}
    clock = {}
    total = {}
    for i in order:
        o = ops[i]
        e = o["eng"]
        need = {}
        for d in o["deps"]:
            s, v = ops[d]["sem"], ops[d]["val"]
            if v > need.get(s, (0, None))[0]:
                need[s] = (v, d)
        for s, (v, d) in sorted(need.items(), key=lambda x: -x[1][1]):
            if seen[e].get(s, 0) < v:
                queue[e].wait_ge(T.sem[s], v)
                seen[e][s] = v
                if not ops[d]["far"]:
                    for s2, v2 in clock[d].items():
                        seen[e][s2] = max(seen[e].get(s2, 0), v2)
        ins = o["fn"]()
        clock[i] = dict(seen[e])
        if o["sem"] is None:
            count[e] += 1
            o["sem"], o["val"] = e, count[e]
            ins.then_inc(T.sem[e], 1)
        elif not o["far"]:
            ins.then_inc(T.sem[o["sem"]], 16)
        total[o["sem"]] = max(total.get(o["sem"], 0), o["val"])
    return total, seen


def rank_program(g, core, T, topo):
    rank = T.rank_of(core)
    if rank is None:
        return
    nxt = T.cores[(rank + 1) % len(T.cores)]
    prv = T.cores[(rank - 1) % len(T.cores)]
    assert topo.may_write(core, nxt)
    rid, pid = topo.addr(nxt)[:2]
    mask = topo.mask(core, nxt)

    def send(out, in_, sem):
        return lambda: g.remote_dma(out, in_, T.sem[sem], T.sem.loc, pid, rid, mask)

    ops = build(g, T, send, len(topo.engines(prv, core)))
    order = schedule(ops)
    total, seen = emit(g, T, ops, order)
    total["loc"] = NS * len(topo.engines(core, nxt))
    for s, v in total.items():
        if all(seen[e].get(s, 0) < v for e in seen):
            g.wait_ge(T.sem[s], v)
